import numpy as np, ml_dtypes
CORES = [8,9,10,11,12,13]
N = 6
BF = ml_dtypes.bfloat16
def gentries(a):
    return np.ascontiguousarray(a.reshape(8, 16, -1).transpose(0, 2, 1)).reshape(8, -1)
def gtable(e):
    e = np.asarray(e); return np.ascontiguousarray(e.reshape(8, -1, 16).transpose(0, 2, 1)).reshape(128, -1).astype(np.int32)
W, L, M, RO = 4096, 128, 32, 5
def base(rng):
    x = rng.integers(0, 256, (N, 8, W, 16)); o = rng.permutation(W); h = W >> 3
    x[:, :, o[:h]] = x[:, :, o[h:2 * h]]
    ring = rng.integers(0, W, (N, 8, 16, L)); o = rng.permutation(L)
    ring[..., o[:4]] = ring[..., o[4:8]]
    return x, ring, rng.integers(0, 32, (N, 8, 16)), rng.integers(0, W >> 1, (N, 8, M))
def pack(x, ring, wt, kap):
    return {"x": np.ascontiguousarray(x.transpose(0, 1, 3, 2)).reshape(N, 128, W).astype(np.float32).astype(BF), "ring": np.ascontiguousarray(ring.reshape(N, 128, L)).astype(np.int32),
            "wt": np.ascontiguousarray(wt.reshape(N, 128, 1)).astype(np.int32), "kap": np.stack([gtable(a) for a in kap])}
def setup_inputs(rng):
    return pack(*base(rng))
def setup_inputs_spread(rng):
    x = np.minimum((np.exp2(8 * rng.random((N, 8, W, 1))) * rng.random((N, 8, W, 16)) * 1.25).astype(np.int64), 255) * (rng.random((N, 8, W, 1)) > 0.0625)
    low = np.minimum((W * rng.random((N, 8, 16, L)) ** 4).astype(np.int64), W - 1)
    ring = np.where(rng.random((N, 8, 1, L)) < 0.5, low, W - 1 - low)
    wt = np.minimum(np.exp2(5.2 * rng.random((N, 8, 16))).astype(np.int64), 31) * (rng.random((N, 8, 16)) > 0.125)
    kap = np.minimum(np.exp2(np.log2(W) * rng.random((N, 8, M))).astype(np.int64) - 1, W // 2 - 1)
    return pack(x, ring, wt, kap)
def setup_inputs_ends(rng):
    x = 255 * rng.integers(0, 2, (N, 8, W, 16)); q = rng.random((N, 8, W)); x[q < 0.25] = 0; x[q >= 0.75] = 255
    wt = 31 * rng.integers(0, 2, (N, 8, 16)); wt[:, 3] = 31; wt[:, 7] = 31; wt[:, 4] = 0
    kap = (W // 2 - 1) * rng.integers(0, 2, (N, 8, M))
    ring = (W - 1) * rng.integers(0, 2, (N, 8, 16, L)); mid = rng.random((N, 8, 16, L)) < 0.2
    for g in (0, 3, 7): mid[:, g] = False
    ring = np.where(mid, rng.integers(0, W, (N, 8, 16, L)), ring)
    c = (((W - 1) ** 2 >> 5) + kap * (W - 1) + (2 * np.arange(M) + 1) * (W - 1)) & (W - 1)
    for r in range(N):
        for g in (0, 3, 7):
            x[r, g, c[r, g]] = 0 if g == 0 else 255
            if g == 3: x[r, g, c[r, g, M - 1], int(rng.integers(0, 16))] = 254
            x[r, g, W - 1] = 0; x[r, g, 0] = 255
            for i in (2, 5, L - 1): ring[r, g, :2, i] = W - 1
            for i in (1, 8, L - 2): ring[r, g, :2, i] = 0
    return pack(x, ring, wt, kap)
def setup_inputs_corners(rng):
    x, ring, wt, kap = base(rng)
    for f_ in (0, 15): x[..., f_] = 32 * rng.integers(0, 8, (N, 8, W)) + rng.choice(np.array([0, 15, 16, 31, 1, 14, 17, 30]), (N, 8, W))
    for r in range(N):
        for g in range(8):
            k = (r + g) % 4; wt[r, g] = 31 if k == 2 else 0
            if k == 0: wt[r, g, 0] = 1
            if k == 3: wt[r, g, 15] = 1
            k = (r + g // 2) % 3; kap[r, g] = 0 if k == 0 else W // 2 - 1 if k == 1 else rng.choice(np.array([0, 1, W // 2 - 2, W // 2 - 1]), M)
    kind = rng.integers(0, 6, (N, 8, 1, L)); turn = (W - 1) * (np.arange(16) & 1)[None, None, :, None]
    ring = np.where(kind == 1, ring[:, :, :1], ring); ring = np.where(kind == 2, 0, ring); ring = np.where(kind == 3, W - 1, ring); ring = np.where(kind == 4, turn, ring)
    return pack(x, ring, wt, kap)
def setup_inputs_crowd(rng):
    x, ring, wt, kap = base(rng); wt[...] = 0; wt[..., 0] = 1; ring = np.minimum(ring, W - 2)
    i = int(rng.choice(np.array([0, L // 2, L - 1]))); sel = rng.integers(0, 4, L); o = 1 + rng.permutation(W - 2)
    for r in range(N):
        k = 3 if r == 3 else r % 3; up = 16 if k < 2 else 0
        x[r, ..., 0] = (x[r, ..., 0] & 3) + 2 if k == 3 else (x[r, ..., 0] & 239) + up
        for g in (0, 1): ring[r, g] = np.repeat(ring[r, g, :, :1].copy(), L, axis=1)
        ring[r, 1, :, i] = rng.integers(0, W - 1, 16)
        ring[r, 4] = ring[r, 4][:, sel]
        for g in (2, 3, 5, 7):
            v = int(rng.integers(1, W - 1)); x[r, g, v] = 0; x[r, g, v, 0] = 5 + up
            ring[r, g, 1] = v; ring[r, g, 5] = 0; kap[r, g] = 0
            if g in (3, 5): ring[r, g, 5, i] = int(rng.integers(1, W - 1))
        x[r, 6, :, 1] &= 127; x[r, 6, 0] = 0; x[r, 6, 0, 1] = 64; x[r, 6, o[0], 0] = 5 + up; x[r, 6, o[1], 0] = 6 + up
        ring[r, 6, 0] = o[0]; ring[r, 6, 1] = o[1]; ring[r, 6, 5] = 0; ring[r, 6, 6] = rng.permutation(o[2:])[:L]
        if k == 1: x[r, 6, W - 1, 0] = 5; ring[r, 6, 0, L - 1] = W - 1
        if k == 3: x[r, 4, W - 1, 0] = 16; ring[r, 4, 1, rng.permutation(L)[:int(rng.integers(1, 64))]] = W - 1
    return pack(x, ring, wt, kap)
def setup_inputs_ties(rng):
    x, ring, wt, kap = base(rng); pool = rng.integers(0, 256, (N, 8, 5, 16)); pool[:, :, 4] = (pool[:, :, 0] + pool[:, :, 1]) & 255
    pool[:, ::2, 3] = pool[:, ::2, 2] ^ 1
    x = np.take_along_axis(pool, rng.integers(0, 5, (N, 8, W, 1)), 2)
    for g in (1, 4, 7):
        ring[:, g] = rng.integers(0, 64, (N, 16, L))
        x[:, g, :64] = rng.integers(0, 4, (N, 64, 16)); x[:, g, 64:] = rng.integers(240, 256, (N, W - 64, 16))
    return pack(x, ring, wt, kap)
def check_inputs(d):
    bad = []
    for k, lo, hi in (("x", 0, 255), ("ring", 0, W - 1), ("wt", 0, 31), ("kap", 0, W // 2 - 1)):
        a = np.asarray(d[k]).astype(np.float32)
        if not (np.min(a) >= lo and np.max(a) <= hi): bad.append("range of " + k)
        elif np.any(a != np.floor(a)): bad.append("whole numbers of " + k)
    return bad
def pick(X, ix):
    return np.take_along_axis(X, ix[..., None], 2)
def reference(x, ring, wt, kap):
    X = np.ascontiguousarray(x.astype(np.float32).astype(np.int32).reshape(N, 8, 16, W).transpose(0, 1, 3, 2))
    R = ring.astype(np.int64).reshape(N, 8, 16, L); wts = wt.astype(np.int32).reshape(N, 8, 1, 16)
    kp = np.stack([gentries(a) for a in kap]).astype(np.int64)[:, :, None, :]; odd = 2 * np.arange(M) + 1
    A = np.zeros(N, np.int64)
    for t in range(RO):
        far = np.stack([R[(r + 1 + t % (N - 1)) % N] for r in range(N)])
        both = np.concatenate([R, far], axis=2)
        a = (np.add.reduce(pick(X, R[:, :, 0]) * wts, axis=3) & 31).astype(np.int64)
        b = (np.add.reduce(pick(X, R[:, :, 1]) * wts, axis=3) & 31).astype(np.int64)
        P = np.take_along_axis(both, a[:, :, None, :], 2)[:, :, 0]; Q = np.take_along_axis(both, b[:, :, None, :], 2)[:, :, 0]
        y = (pick(X, P) + pick(X, Q)) & 255
        c = (((P * Q) >> 5)[..., None] + kp * P[..., None] + odd * Q[..., None] + A[:, None, None, None]) & (W - 1)
        s = np.add.reduce(np.abs(pick(X, c.reshape(N, 8, L * M)).reshape(N, 8, L, M, 16) - y[:, :, :, None, :]), axis=4)
        m = np.argmin(s, axis=3)
        e = np.take_along_axis(c, m[..., None], 3)[..., 0]
        A = np.add.reduce(((a >= 16).astype(np.int64) + (b >= 16)).reshape(N, 8 * L), axis=1) & 63
        for r in range(N):
            for g in range(8):
                v, i = np.unique(e[r, g], return_index=True)
                X[r, g, v] = (X[r, g, v] + y[r, g, i]) >> 1
        R = np.concatenate([e[:, :, None, :], R[:, :, :15]], axis=2)
    return {"yx": np.ascontiguousarray(X.transpose(0, 1, 3, 2)).reshape(N, 128, W).astype(np.float32).astype(BF), "yr": R.reshape(N, 128, L).astype(np.float32)}

@@ -1,0 +1,457 @@
+import numpy as np
+from concourse.mybir import AluOpType as OP, ActivationFunctionType as AF
+
+W, L, M, RO, N = 4096, 128, 32, 5, 6
+BIG = float(1 << 22)
+R1 = float(3 << 22)
+R64 = float(3 << 28)
+V_LAG, LATE = 400, 200
+KP_S = [[0, 1], [2, 3], []]
+S_CH = [4, 4, 4, 2]
+V_CH = [4, 4, 4, 4, 2]
+F, B16, I32, U16 = "float32", "bfloat16", "int32", "uint16"
+
+
+def _sb(cols, dt_):
+    return ("sbuf", [128] + (cols if isinstance(cols, list) else [cols]), dt_)
+
+
+SCRATCH = {
+    "X": _sb(W + L, B16), "win": _sb(RO * 256, F), "h16": _sb(56, U16),
+    "rin": _sb(128, I32), "rf": _sb(256, F), "rt": _sb(256, F), "wti": _sb(4, I32), "kpi": _sb(4, I32),
+    "pc": _sb(16, I32), "pf": _sb(16, F), "pi": _sb(128, I32), "pj": _sb(128, I32), "j8": _sb(8, F),
+    "lt": _sb(8, U16), "cexp": _sb(8, U16), "jg": _sb(128, B16), "i8m": _sb(256, B16), "tg": _sb(128, B16),
+    "km": _sb(32, F), "kf": _sb(4, F), "wf": _sb(4, F),
+    "idn": _sb(128, B16), "nid": _sb(128, B16), "n128": _sb(128, B16), "dm": _sb(256, F), "nb": _sb(128, B16),
+    "bb": _sb(128, B16), "bf": _sb(128, F), "tri": _sb(128, B16), "wb": _sb(512, B16), "b8": _sb(32, B16),
+    "i4": _sb(64, F), "j4": _sb(64, B16), "nb4": _sb(64, B16), "rs4": _sb(64, F),
+    "rst": _sb(256, F), "rk": _sb(256, F), "d0": _sb(128, F), "ck": _sb(256, B16), "odd": _sb(32, F),
+    "kr": _sb(32, F), "fw": _sb(256, B16), "o16": _sb(128, F), "half": _sb(128, B16),
+    "xab": _sb(256, B16), "sa": _sb(64, F), "ai": _sb(16, I32), "aj": _sb(16, I32), "ao": _sb(16, U16),
+    "mpq": _sb(256, F), "spq": _sb(256, F), "opq": _sb(16, U16), "pqi": _sb(8, I32), "fi": _sb(8, I32),
+    "gg": _sb(8, F), "t1": _sb(256, F), "ci": _sb(256, I32), "cm": _sb(256, I32), "co": _sb(256, U16),
+    "junk": _sb(256, F), "cnt": _sb(4, F), "aq": _sb(4, F), "ar": _sb(4, F), "ac": _sb(4, F),
+    "xpq": _sb(256, B16), "sg": _sb(128, B16), "yy": _sb(512, B16),
+    "dd": _sb(W, B16), "rl": _sb(W, B16),
+    "sk": _sb(256, F), "ki": _sb(8, I32), "kj": _sb(8, I32), "ex": _sb(128, B16), "eo": _sb(8, U16),
+    "me": _sb(128, F), "se": _sb(128, F), "cmp": _sb([8, 128], B16), "sc": _sb(128, F), "so": _sb(8, U16),
+    "xe": _sb(128, B16), "uu": _sb(128, F), "nv": _sb(128, B16), "er": _sb(RO * 128, F),
+}
+for _k in range(8):
+    SCRATCH["ps%d" % _k] = ("psum", [128, 512], F)
+
+SEMAPHORES = ["cV", "cS", "cP", "cG", "sent"] + ["arr%d" % _t for _t in range(RO)] + ["dq%d" % _k for _k in range(24)]
+
+
+def rank_program(g, core, T, topo):
+    rank = T.rank_of(core)
+    if rank is None:
+        return
+    ops = []
+    ALL = slice(None)
+
+    def cols(a):
+        name, idx = a[0], a[1]
+        shape = SCRATCH[name][1][1:]
+        m = np.zeros(shape, bool)
+        m[idx[1:]] = True
+        return m.reshape(-1)
+
+    def A(name, lo=None, hi=None, step=None):
+        return (name, (ALL, slice(lo, hi, step)))
+
+    def ind(win, off):
+        return (win[0], win[1], off)
+
+    def ap(a):
+        if not isinstance(a, tuple):
+            return a
+        v = T[a[0]][a[1]]
+        return v.indirect(ap(a[2])) if len(a) == 3 else v
+
+    def add(eng, call, outs, ins, dma=False, after=(), waits=()):
+        rd, wr = [], []
+        for a in ins:
+            if isinstance(a, tuple):
+                rd.append((a[0], cols(a)))
+                if len(a) == 3:
+                    rd.append((a[2][0], cols(a[2])))
+        for a in outs:
+            wr.append((a[0], cols(a)))
+            if len(a) == 3:
+                rd.append((a[2][0], cols(a[2])))
+        ops.append({"eng": eng, "call": call, "rd": rd, "wr": wr, "dma": dma, "after": list(after), "waits": list(waits)})
+        return len(ops) - 1
+
+    V, S, P = g.vector, g.scalar, g.tensor
+
+    def copy(o, i):
+        return add("V", lambda: V.tensor_copy(ap(o), ap(i)), [o], [i])
+
+    def tt(o, a, b, op, waits=()):
+        return add("V", lambda: V.tensor_tensor(ap(o), ap(a), ap(b), op), [o], [a, b], waits=waits)
+
+    def ts(o, a, s1, op0, s2=None, op1=None):
+        if op1 is None:
+            return add("V", lambda: V.tensor_scalar(ap(o), ap(a), ap(s1), None, op0), [o], [a, s1])
+        return add("V", lambda: V.tensor_scalar(ap(o), ap(a), ap(s1), ap(s2), op0, op1), [o], [a, s1, s2])
+
+    def scan(o, d0, d1, op0, op1):
+        return add("V", lambda: V.tensor_tensor_scan(ap(o), ap(d0), ap(d1), 0.0, op0, op1), [o], [d0, d1])
+
+    def fill(o, c):
+        return add("V", lambda: V.memset(ap(o), c), [o], [])
+
+    def act(o, i, f=AF.Identity, bias=0.0, scale=1.0, acc=None):
+        if acc is None:
+            return add("S", lambda: S.activation(ap(o), ap(i), f, bias=ap(bias), scale=ap(scale)), [o], [i, bias, scale])
+        return add("S", lambda: S.activation(ap(o), ap(i), f, bias=ap(bias), scale=ap(scale), accum_out=ap(acc)),
+                   [o, acc], [i, bias, scale])
+
+    def mm(o, l, r, start, stop):
+        return add("P", lambda: P.matmul(ap(o), ap(l), ap(r), start, stop), [o], [l, r])
+
+    def iota(o, pat, base, cm):
+        if SCRATCH[o[0]][2] == I32:
+            return add("G", lambda: g.iota(ap(o), pat, base, cm), [o], [])
+        return add("G", lambda: g.iota(ap(o), pat, base, cm, allow_small_or_imprecise_dtypes=True), [o], [])
+
+    def dma(q, o, i, after=()):
+        Q = {"Y": g.sync, "S": g.scalar}[q]
+        return add(q, lambda: Q.dma_start(ap(o), ap(i)), [o] if isinstance(o, tuple) else [], [i], dma=True, after=after)
+
+    sent = [0]
+
+    def engines(src, dst, kind):
+        es = topo.engines(src, dst)
+        return (es[0::2], es[1::2], es)[kind]
+
+    def send(kind, t, dst, src, after=()):
+        peer = T.cores[(rank - 1 - t) % N]
+        rid, pid, _se = topo.addr(peer)
+        es = engines(core, peer, kind)
+        mask = sum(1 << e for e in es)
+        sent[0] += len(es)
+        add("G", lambda: g.remote_dma(ap(dst), ap(src), T.sem["arr%d" % t], T.sem.sent, pid, rid, mask), [], [src],
+            dma="remote", after=after)
+
+    def arrivals(t):
+        return sum(len(engines(T.cores[(rank + 1 + t) % N], core, kind)) for kind in ((0,) if t == 0 else (1, 2)))
+
+    col = lambda name, j: A(name, j, j + 1)
+    XW = A("X", 0, W)
+
+    dma("Y", A("rin"), T.ring[:])
+    dma("Y", XW, T.x[:])
+    dma("S", A("kpi", 0, 2), T.kap[:])
+    dma("S", A("wti", 0, 1), T.wt[:])
+
+    iota(col("pc", 0), [[0, 1]], 0, 1)
+    iota(A("j8"), [[1, 8]], 0, 0)
+    iota(A("pi"), [[1, 128]], 0, -1)
+    iota(A("jg"), [[1, 8], [0, 16]], 0, 0)
+    iota(A("i4"), [[0, 16], [1, 4]], 0, 0)
+    iota(A("j4"), [[0, 2], [1, 8], [0, 4]], 0, 0)
+    iota(A("odd"), [[2, 32]], 1, 0)
+    iota(A("i8m"), [[0, 8], [8, 32]], 0, 0)
+    fill(A("half"), -0.5)
+    fill(A("X", W, W + L), 0.0)
+    act(A("fw", 0, 128), A("half"), scale=0.0)
+    act(A("fw", 128, 256), A("half"), scale=-2.0)
+    act(A("o16"), A("half"), scale=-0.125)
+    act(A("rk", 0, 128), A("half"), scale=0.0)
+    act(A("rk", 128, 256), A("half"), scale=0.0)
+    act(A("d0"), A("half"), scale=0.0)
+    act(A("rk", 0, 256, 32), A("half", 0, 8), scale=-2.0 * BIG)
+    ts(col("pc", 1), col("pc", 0), 4, OP.arith_shift_right, 1, OP.bitwise_and)
+    ts(col("pc", 2), col("pc", 0), 3, OP.arith_shift_right, 1, OP.bitwise_and)
+    ts(col("pc", 3), col("pc", 0), 4, OP.arith_shift_right)
+    ts(col("pc", 4), col("pc", 0), 15, OP.bitwise_and)
+    ts(col("pc", 5), col("pc", 0), 2, OP.arith_shift_right, 3, OP.bitwise_and)
+    tt(col("pc", 8), col("pc", 0), col("pc", 1), OP.subtract)
+    copy(A("pf", 0, 6), A("pc", 0, 6))
+    ts(col("pc", 6), col("pc", 8), 7, OP.bitwise_and)
+    ts(col("pc", 7), col("pc", 8), 1, OP.bitwise_and)
+    copy(A("cexp"), A("j8"))
+    ts(col("pf", 6), col("pc", 6), col("pf", 1), OP.add, 16.0, OP.mult)
+    ts(col("pf", 7), col("pc", 7), 112.0, OP.mult, col("pf", 2), OP.add)
+    ts(A("pj"), A("pi"), 15, OP.bitwise_and)
+    tt(col("pf", 8), col("pf", 6), col("pf", 7), OP.add)
+    ts(A("idn"), A("pi"), 0.0, OP.is_equal)
+    ts(A("lt"), A("j8"), 2.0, OP.mult, col("pf", 8), OP.add)
+    ts(A("bb"), A("jg", 0, 128), col("pf", 3), OP.is_equal)
+    ts(A("dm", 0, 128), A("pj"), 0.0, OP.is_equal)
+    fill(A("wb"), 0.0)
+    ts(A("nb4"), A("i4"), col("pf", 5), OP.not_equal, -BIG, OP.mult)
+    ts(A("rs4"), A("i4"), 1.0, OP.min)
+    copy(A("rf", 0, 128), A("rin"))
+    copy(A("rf", 128, 240), A("rin", 16, 128))
+    copy(A("rf", 240, 256), A("rin", 0, 16))
+    add("V", lambda: V.transpose(ap(A("rt")), ap(A("rf"))), [A("rt")], [A("rf")])
+    ts(col("wf", 0), col("wti", 0), 8.0, OP.mult)
+    copy(A("win", 0, 128), ind(A("rt"), A("lt")))
+    send(0, 0, A("win", 128, 256), A("win", 0, 128))
+    copy(A("kf", 0, 2), A("kpi", 0, 2))
+    copy(A("h16", 40, 56), A("win", 0, 16))
+    act(A("bf"), A("bb"))
+    act(A("dm", 128, 256), A("dm", 0, 128))
+    act(A("nb"), A("dm", 0, 128), bias=-BIG, scale=BIG)
+    act(A("nid"), A("idn"), scale=-1.0)
+    act(A("n128"), A("idn"), scale=-128.0)
+    for q in range(4):
+        act(A("wb", 129 * q, 128 * q + 128, 4), A("bb", q, 128, 4), scale=col("wf", 0))
+    ts(A("km", 0, 16), A("dm", 0, 16), col("kf", 0), OP.mult)
+    ts(A("km", 16, 32), A("dm", 0, 16), col("kf", 1), OP.mult)
+    fill(A("rst"), 1.0)
+    add("G", lambda: g.affine_select(ap(A("tri")), ap(A("bb")), [[1, 128]], OP.is_gt, 0.0, 0, -1), [A("tri")], [A("bb")])
+    mm(A("ps7", 0, 32), A("bf"), A("km"), True, True)
+    PA = A("ps0", 0, 64)
+
+    def age_const():
+        mm(PA, A("idn"), A("nb4"), True, False)
+        mm(PA, A("idn"), A("j4"), False, False)
+
+    age_const()
+    act(A("b8", 0, 8), A("bb", 0, 128, 16))
+    act(A("b8", 8, 16), A("bb", 0, 128, 16), scale=256.0)
+    act(A("b8", 16, 24), A("bb", 0, 128, 16), scale=512.0)
+    act(A("b8", 24, 32), A("bb", 0, 128, 16), scale=-256.0)
+    act(A("kr"), A("ps7", 0, 32))
+    ts(col("pf", 9), col("pf", 4), float(W), OP.add)
+    ts(A("ck"), A("i8m"), col("pf", 3), OP.add)
+    fill(A("rst", 0, 256, 16), 0.0)
+    ts(A("d0", 0, 128, 16), A("j8"), 16.0, OP.mult, col("pf", 9), OP.add)
+
+    PT, PC, PK = A("ps1", 0, 256), A("ps1", 0, 128), A("ps2", 0, 256)
+    PY1, PW, PY2, PE_ = A("ps3", 0, 128), A("ps3", 0, 8), A("ps4", 0, 256), A("ps4", 0, 128)
+    PN, PCNT = A("ps7", 0, 128), A("ps7", 0, 1)
+    diag = lambda name, n: A(name, 15, n, 16)
+
+    for t in range(RO):
+        last = t == RO - 1
+        w0 = 256 * t
+        h0 = 8 * (RO - t)
+        copy(A("xab", 0, 128), ind(XW, A("h16", h0, h0 + 8)))
+        act(A("xab", 128, 256), ind(XW, A("h16", h0 + 8, h0 + 16)))
+        for q in range(4):
+            mm(PA, A("wb", 128 * q, 128 * q + 128), A("xab", q, 256, 4), False, q == 3)
+        scan(A("sa"), A("rs4"), PA, OP.mult, OP.max)
+        copy(A("ai"), A("sa", 3, 64, 4))
+        ts(A("aj"), A("ai"), 255, OP.bitwise_and)
+        copy(A("ao"), A("aj"))
+        tt(A("mpq"), ind(A("win", w0, w0 + 256), A("ao")), A("dm"), OP.mult, waits=[("arr%d" % t, arrivals(t))])
+        if not last:
+            act(A("junk"), ind(A("fw"), A("ao")), bias=-63.0 / 4096, acc=col("cnt", 0))
+        spq = scan(A("spq"), A("rst"), A("mpq"), OP.mult, OP.max)
+        if t == 0:
+            old = dma("Y", T.yr[RO:128, :], ("rf", (slice(0, 128 - RO), slice(0, 128))), after=[spq])
+        if not last:
+            mm(PCNT, A("o16"), col("cnt", 0), True, True)
+            dma("Y", A("win", w0 + 264, w0 + 384), A("win", w0, w0 + 120), after=[spq])
+            send(1, t + 1, A("win", w0 + 256 + 136, w0 + 512), A("win", w0, w0 + 120), after=[spq])
+        Pc = lambda ii: col("spq", 16 * ii + 15)
+        Qc = lambda ii: col("spq", 128 + 16 * ii + 15)
+        kp_s = lambda ii: act(A("t1", ii, 256, 8), A("kr"), scale=Pc(ii))
+        kp_v = lambda ii: ts(A("t1", ii, 256, 8), A("kr"), Pc(ii), OP.mult)
+        kv = [ii for ii in range(8) if ii not in sum(KP_S, [])]
+        copy(A("opq"), diag("spq", 256))
+        for ii in KP_S[0]:
+            kp_s(ii)
+        tt(A("pqi"), A("spq", 15, 128, 16), A("spq", 143, 256, 16), OP.mult)
+        act(A("xpq"), ind(XW, A("opq")))
+        kp_v(kv[0])
+        ts(A("fi"), A("pqi"), 5, OP.arith_shift_right)
+        kp_v(kv[1])
+        if t == 0:
+            copy(A("gg"), A("fi"))
+        else:
+            ts(A("gg"), A("fi"), col("ac", 0), OP.add, 31.5, OP.add)
+        for ii in kv[2:]:
+            kp_v(ii)
+        mm(PY1, A("idn"), A("xpq", 0, 128), True, False)
+        mm(PY1, A("idn"), A("xpq", 128, 256), False, True)
+        mm(PY2, A("idn"), A("xpq"), True, False)
+        mm(A("ps4", 0, 128), A("idn"), A("xpq", 128, 256), False, False)
+        mm(A("ps4", 128, 256), A("idn"), A("xpq", 0, 128), False, False)
+        for ii in KP_S[1]:
+            kp_s(ii)
+        act(A("sg"), PY1, AF.Sign, bias=-255.5)
+        for ii in KP_S[2]:
+            kp_s(ii)
+        for k in range(2):
+            mm(A("ps4", 128 * k, 128 * k + 128), A("n128"), A("sg"), False, k == 1)
+        for ii in range(8):
+            ts(A("ps1", ii, 256, 8), A("odd"), Qc(ii), OP.mult, col("gg", ii), OP.add)
+        act(A("yy", 0, 256), PY2, bias=-128.0)
+        mm(PK, A("idn"), A("ck"), True, False)
+        tt(A("ci", 0, 64), A("t1", 0, 64), A("ps1", 0, 64), OP.add)
+        tt(A("ci", 64, 256), A("t1", 64, 256), A("ps1", 64, 256), OP.add)
+        ts(A("cm", 0, 64), A("ci", 0, 64), W - 1, OP.bitwise_and)
+        ts(A("cm", 64, 256), A("ci", 64, 256), W - 1, OP.bitwise_and)
+        copy(A("co", 0, 64), A("cm", 0, 64))
+        copy(A("yy", 256, 512), A("yy", 0, 256))
+        copy(A("co", 64, 256), A("cm", 64, 256))
+        sm = [sum(S_CH[:k]) for k in range(len(S_CH) + 1)]
+        vm = [sm[-1] + sum(V_CH[:k]) for k in range(len(V_CH) + 1)]
+        left = [sum(S_CH) + 2 * sum(V_CH)]
+
+        def keys(buf, m0, m1, c):
+            for m in range(m0, m1):
+                left[0] -= 1
+                mm(A("ps2", m, 256, 32), A(buf, 128 * m, 128 * m + 128), A("b8", c, c + 8), False, left[0] == 0)
+
+        def s_gather(k):
+            act(A("dd", 128 * sm[k], 128 * sm[k + 1]), ind(XW, A("co", 8 * sm[k], 8 * sm[k + 1])))
+
+        def s_sub(k):
+            a, n, bank = sm[k], 128 * S_CH[k], "ps%d" % (5 + k % 2)
+            mm(A(bank, 0, n), A("idn"), A("dd", 128 * a, 128 * a + n), True, False)
+            for c in range(0, n, 256):
+                d = min(c + 256, n)
+                mm(A(bank, c, d), A("nid"), A("yy", 0, d - c), False, d == n)
+
+        def s_abs(k):
+            act(A("rl", 128 * sm[k], 128 * sm[k + 1]), A("ps%d" % (5 + k % 2), 0, 128 * S_CH[k]), AF.Abs)
+
+        def v_gather(k):
+            a, b = vm[k], vm[k + 1]
+            tt(A("dd", 128 * a, 128 * b), ind(XW, A("co", 8 * a, 8 * b)), A("yy", 0, 128 * (b - a)), OP.subtract)
+
+        def v_relu(k):
+            ts(A("rl", 128 * vm[k], 128 * vm[k + 1]), A("dd", 128 * vm[k], 128 * vm[k + 1]), 0.0, OP.max)
+
+        def consts():
+            mm(PC, A("nid"), A("nb"), True, False)
+            if not last:
+                age_const()
+
+        turns = lambda n: [("g", 0)] + sum([[("g", k + 1), ("a", k)] for k in range(n - 1)], []) + [("a", n - 1)]
+        ev, ts_, tv = [(1, 0, consts)], 0, V_LAG
+        for w, k in turns(len(S_CH)):
+            if w == "g":
+                ev.append((ts_, 0, lambda k=k: s_gather(k)))
+                ts_ += 60 + 200 * S_CH[k]
+                ev.append((ts_, 1, lambda k=k: s_sub(k)))
+            else:
+                ev.append((ts_, 2, lambda k=k: s_abs(k)))
+                ts_ += 60 + 128 * S_CH[k]
+                ev.append((ts_ + LATE, 3, lambda k=k: keys("rl", sm[k], sm[k + 1], 8)))
+        for w, k in turns(len(V_CH)):
+            if w == "g":
+                ev.append((tv, 0, lambda k=k: v_gather(k)))
+                tv += 50 + 200 * V_CH[k]
+                ev.append((tv + LATE, 3, lambda k=k: keys("dd", vm[k], vm[k + 1], 24)))
+            else:
+                ev.append((tv, 2, lambda k=k: v_relu(k)))
+                tv += 64 * V_CH[k]
+                ev.append((tv + LATE, 3, lambda k=k: keys("rl", vm[k], vm[k + 1], 16)))
+        for e_ in sorted(ev, key=lambda x: x[:2]):
+            e_[2]()
+        scan(A("sk"), A("rk"), PK, OP.add, OP.min)
+        if not last:
+            act(col("aq", 0), PCNT, bias=R64)
+            act(col("ar", 0), col("aq", 0), bias=R64, scale=-1.0)
+            act(col("ac", 0), PCNT, bias=col("ar", 0))
+        copy(A("ki"), A("sk", 31, 256, 32))
+        ts(A("kj"), A("ki"), 255, OP.bitwise_and)
+        tt(A("ex"), ind(A("kj"), A("cexp")), A("dm", 0, 128), OP.mult)
+        mm(PW, A("ex"), A("b8", 0, 8), True, True)
+        mm(PN, A("idn"), A("half"), True, False)
+        mm(PN, A("idn"), A("yy", 0, 128), False, False)
+        copy(A("eo"), PW)
+        tt(A("me"), ind(A("cm"), A("eo")), A("dm", 0, 128), OP.mult)
+        mm(PE_, A("bf"), A("me"), True, True)
+        mm(PC, A("bf"), A("me"), False, False)
+        scan(A("se"), A("rst", 0, 128), A("me"), OP.mult, OP.max)
+        copy(A("h16", h0 - 8, h0), diag("se", 128))
+        if not last:
+            act(A("win", w0 + 256, w0 + 264), diag("se", 128))
+            send(2, t + 1, A("win", w0 + 256 + 128, w0 + 256 + 136), A("win", w0 + 256, w0 + 264))
+        act(A("xe"), ind(XW, A("h16", h0 - 8, h0)))
+        for ii in range(8):
+            n = 128 - 16 * ii
+            ts(("cmp", (ALL, ii, slice(0, n))), A("ps4", 16 * ii, 128), col("se", 16 * ii + 15), OP.is_equal, 8192.0, OP.mult)
+            if ii < 7:
+                mm(A("ps1", 16 * ii + 16, 128), A("bb"), ("cmp", (ALL, ii, slice(16, n))), False, False)
+            if ii == 2:
+                mm(PN, A("idn"), A("xe"), False, True)
+        mm(PC, A("tri"), ("cmp", (ALL, ALL, slice(0, 16))), False, True)
+        act(A("uu"), PN, bias=R1, scale=0.5)
+        act(A("nv"), A("uu"), bias=-R1)
+        scan(A("sc"), A("d0"), PC, OP.max, OP.min)
+        copy(A("so"), diag("sc", 128))
+        act(A("er", 128 * t, 128 * t + 128), PE_)
+        copy(ind(A("X"), A("so")), A("nv"))
+        if last:
+            dma("Y", T.yx[:], XW)
+        dma("Y", T.yr[RO - 1 - t:128:16, :], ("er", (slice(0, 128, 16), slice(128 * t, 128 * t + 128))), after=[old])
+
+    emit(g, T, ops, sent[0])
+
+
+def emit(g, T, ops, sent):
+    Q = {"V": g.vector, "S": g.scalar, "P": g.tensor, "G": g, "Y": g.sync}
+    seen, know, seq, ndma = {}, {k: {} for k in Q}, {k: 0 for k in Q}, 0
+    for n, o in enumerate(ops):
+        e = o["eng"]
+        deps = set(o["after"])
+        for kind in ("rd", "wr"):
+            for name, m in o[kind]:
+                for (k, km, kw) in seen.get(name, []):
+                    other = ops[k]["eng"] != e or ops[k]["dma"] or o["dma"]
+                    if name.startswith("ps") and other:
+                        deps.add(k)
+                    elif (kw or kind == "wr") and (m & km).any() and not (e == "P" and not other):
+                        deps.add(k)
+        need = {}
+        for k in deps:
+            if ops[k]["dma"] == "remote":
+                continue
+            key, val = ops[k]["id"]
+            if know[e].get(key, 0) < val and need.get(key, (0, 0))[0] < val:
+                need[key] = (val, k)
+        for key in list(need):
+            val, k = need[key]
+            if any(k2 != k and ops[k2]["done"].get(key, 0) >= val for (_v, k2) in need.values()):
+                del need[key]
+        o["need"] = [k for (_v, k) in need.values()]
+        for k in o["need"]:
+            ops[k]["signal"] = True
+            for key, val in ops[k]["done"].items():
+                if know[e].get(key, 0) < val:
+                    know[e][key] = val
+        if o["dma"] == "remote":
+            o["id"] = None
+        elif o["dma"]:
+            o["id"] = ("dq%d" % ndma, 1)
+            ndma += 1
+        else:
+            seq[e] += 1
+            o["id"] = ("c" + e, seq[e])
+        o["done"] = dict(know[e])
+        if o["id"]:
+            o["done"][o["id"][0]] = o["id"][1]
+        for kind in ("rd", "wr"):
+            for name, m in o[kind]:
+                seen.setdefault(name, []).append((n, m, kind == "wr"))
+    count = {k: 0 for k in Q}
+    for o in ops:
+        q = Q[o["eng"]]
+        for k in o["need"]:
+            q.wait_ge(T.sem[ops[k]["id"][0]], ops[k]["val"])
+        for name, val in o["waits"]:
+            q.wait_ge(T.sem[name], val)
+        r = o["call"]()
+        if o["dma"] == "remote":
+            continue
+        if o["dma"]:
+            o["val"] = 16
+            r.then_inc(T.sem[o["id"][0]], 16)
+        elif o.get("signal"):
+            count[o["eng"]] += 1
+            o["val"] = count[o["eng"]]
+            r.then_inc(T.sem[o["id"][0]], 1)
+    g.wait_ge(T.sem.sent, sent)
+    for o in ops:
+        if o["dma"] is True and not o.get("signal"):
+            g.wait_ge(T.sem[o["id"][0]], 16)

@@ -5,10 +5,11 @@ W, L, M, RO, N = 4096, 128, 32, 5, 6
 BIG = float(1 << 22)
 R1 = float(3 << 22)
 R64 = float(3 << 28)
-V_LAG, LATE = 400, 200
-KP_S = [[0, 1], [2, 3], []]
+V_LAG, LATE, END = 100, 200, 1000
+C_CUT = [0, 64, 128, 192, 256]
+Q_S = 2
 S_CH = [4, 4, 4, 2]
-V_CH = [4, 4, 4, 4, 2]
+V_CH = [2, 4, 4, 4, 3, 1]
 F, B16, I32, U16 = "float32", "bfloat16", "int32", "uint16"
 
 
@@ -27,13 +28,13 @@ SCRATCH = {
     "i4": _sb(64, F), "j4": _sb(64, B16), "nb4": _sb(64, B16), "rs4": _sb(64, F),
     "rst": _sb(256, F), "rk": _sb(256, F), "d0": _sb(128, F), "ck": _sb(256, B16), "odd": _sb(32, F),
     "kr": _sb(32, F), "fw": _sb(256, B16), "o16": _sb(128, F), "half": _sb(128, B16),
-    "xab": _sb(256, B16), "sa": _sb(64, F), "ai": _sb(16, I32), "aj": _sb(16, I32), "ao": _sb(16, U16),
+    "xab": _sb(256, B16), "sa": _sb(64, I32), "aj": _sb(16, I32), "ao": _sb(16, U16),
     "mpq": _sb(256, F), "spq": _sb(256, F), "opq": _sb(16, U16), "pqi": _sb(8, I32), "fi": _sb(8, I32),
     "gg": _sb(8, F), "t1": _sb(256, F), "ci": _sb(256, I32), "cm": _sb(256, I32), "co": _sb(256, U16),
     "junk": _sb(256, F), "cnt": _sb(4, F), "aq": _sb(4, F), "ar": _sb(4, F), "ac": _sb(4, F),
     "xpq": _sb(256, B16), "sg": _sb(128, B16), "yy": _sb(512, B16),
     "dd": _sb(W, B16), "rl": _sb(W, B16),
-    "sk": _sb(256, F), "ki": _sb(8, I32), "kj": _sb(8, I32), "ex": _sb(128, B16), "eo": _sb(8, U16),
+    "sk": _sb(256, I32), "kj": _sb(8, I32), "ex": _sb(128, B16), "eo": _sb(8, U16),
     "me": _sb(128, F), "se": _sb(128, F), "cmp": _sb([8, 128], B16), "sc": _sb(128, F), "so": _sb(8, U16),
     "xe": _sb(128, B16), "uu": _sb(128, F), "nv": _sb(128, B16), "er": _sb(RO * 128, F),
 }
@@ -236,61 +237,62 @@ def rank_program(g, core, T, topo):
         for q in range(4):
             mm(PA, A("wb", 128 * q, 128 * q + 128), A("xab", q, 256, 4), False, q == 3)
         scan(A("sa"), A("rs4"), PA, OP.mult, OP.max)
-        copy(A("ai"), A("sa", 3, 64, 4))
-        ts(A("aj"), A("ai"), 255, OP.bitwise_and)
+        ts(A("aj"), A("sa", 3, 64, 4), 255, OP.bitwise_and)
         copy(A("ao"), A("aj"))
-        tt(A("mpq"), ind(A("win", w0, w0 + 256), A("ao")), A("dm"), OP.mult, waits=[("arr%d" % t, arrivals(t))])
+        tt(A("mpq", 0, 128), ind(A("win", w0, w0 + 256), A("ao", 0, 8)), A("dm", 0, 128), OP.mult,
+           waits=[("arr%d" % t, arrivals(t))])
+        tt(A("mpq", 128, 256), ind(A("win", w0, w0 + 256), A("ao", 8, 16)), A("dm", 0, 128), OP.mult)
         if not last:
             act(A("junk"), ind(A("fw"), A("ao")), bias=-63.0 / 4096, acc=col("cnt", 0))
-        spq = scan(A("spq"), A("rst"), A("mpq"), OP.mult, OP.max)
+        Pc = lambda ii: col("spq", 16 * ii + 15)
+        Qc = lambda ii: col("spq", 128 + 16 * ii + 15)
+        kp = lambda ii: ts(A("ps1", ii, 256, 8), A("kr"), Pc(ii), OP.mult)
+        scan(A("spq", 0, 128), A("rst", 0, 128), A("mpq", 0, 128), OP.mult, OP.max)
+        spq = scan(A("spq", 128, 256), A("rst", 0, 128), A("mpq", 128, 256), OP.mult, OP.max)
+        kp(0)
+        copy(A("opq", 0, 8), diag("spq", 128))
+        act(A("xpq", 0, 128), ind(XW, A("opq", 0, 8)))
+        kp(1)
         if t == 0:
             old = dma("Y", T.yr[RO:128, :], ("rf", (slice(0, 128 - RO), slice(0, 128))), after=[spq])
         if not last:
             mm(PCNT, A("o16"), col("cnt", 0), True, True)
             dma("Y", A("win", w0 + 264, w0 + 384), A("win", w0, w0 + 120), after=[spq])
             send(1, t + 1, A("win", w0 + 256 + 136, w0 + 512), A("win", w0, w0 + 120), after=[spq])
-        Pc = lambda ii: col("spq", 16 * ii + 15)
-        Qc = lambda ii: col("spq", 128 + 16 * ii + 15)
-        kp_s = lambda ii: act(A("t1", ii, 256, 8), A("kr"), scale=Pc(ii))
-        kp_v = lambda ii: ts(A("t1", ii, 256, 8), A("kr"), Pc(ii), OP.mult)
-        kv = [ii for ii in range(8) if ii not in sum(KP_S, [])]
-        copy(A("opq"), diag("spq", 256))
-        for ii in KP_S[0]:
-            kp_s(ii)
+        copy(A("opq", 8, 16), A("spq", 143, 256, 16))
         tt(A("pqi"), A("spq", 15, 128, 16), A("spq", 143, 256, 16), OP.mult)
-        act(A("xpq"), ind(XW, A("opq")))
-        kp_v(kv[0])
+        act(A("xpq", 128, 256), ind(XW, A("opq", 8, 16)))
+        for ii in (2, 3, 4):
+            kp(ii)
         ts(A("fi"), A("pqi"), 5, OP.arith_shift_right)
-        kp_v(kv[1])
+        for ii in (5, 6, 7):
+            kp(ii)
         if t == 0:
             copy(A("gg"), A("fi"))
         else:
             ts(A("gg"), A("fi"), col("ac", 0), OP.add, 31.5, OP.add)
-        for ii in kv[2:]:
-            kp_v(ii)
         mm(PY1, A("idn"), A("xpq", 0, 128), True, False)
         mm(PY1, A("idn"), A("xpq", 128, 256), False, True)
         mm(PY2, A("idn"), A("xpq"), True, False)
         mm(A("ps4", 0, 128), A("idn"), A("xpq", 128, 256), False, False)
         mm(A("ps4", 128, 256), A("idn"), A("xpq", 0, 128), False, False)
-        for ii in KP_S[1]:
-            kp_s(ii)
+        for ii in range(Q_S):
+            act(A("t1", ii, 256, 8), A("odd"), scale=Qc(ii), bias=col("gg", ii))
         act(A("sg"), PY1, AF.Sign, bias=-255.5)
-        for ii in KP_S[2]:
-            kp_s(ii)
         for k in range(2):
             mm(A("ps4", 128 * k, 128 * k + 128), A("n128"), A("sg"), False, k == 1)
-        for ii in range(8):
-            ts(A("ps1", ii, 256, 8), A("odd"), Qc(ii), OP.mult, col("gg", ii), OP.add)
+        for ii in range(Q_S, 8):
+            ts(A("t1", ii, 256, 8), A("odd"), Qc(ii), OP.mult, col("gg", ii), OP.add)
         act(A("yy", 0, 256), PY2, bias=-128.0)
         mm(PK, A("idn"), A("ck"), True, False)
-        tt(A("ci", 0, 64), A("t1", 0, 64), A("ps1", 0, 64), OP.add)
-        tt(A("ci", 64, 256), A("t1", 64, 256), A("ps1", 64, 256), OP.add)
-        ts(A("cm", 0, 64), A("ci", 0, 64), W - 1, OP.bitwise_and)
-        ts(A("cm", 64, 256), A("ci", 64, 256), W - 1, OP.bitwise_and)
-        copy(A("co", 0, 64), A("cm", 0, 64))
+        parts = list(zip(C_CUT[:-1], C_CUT[1:]))
+        for a, b in parts:
+            tt(A("ci", a, b), A("t1", a, b), A("ps1", a, b), OP.add)
+        for a, b in parts:
+            ts(A("cm", a, b), A("ci", a, b), W - 1, OP.bitwise_and)
+        for a, b in parts:
+            copy(A("co", a, b), A("cm", a, b))
         copy(A("yy", 256, 512), A("yy", 0, 256))
-        copy(A("co", 64, 256), A("cm", 64, 256))
         sm = [sum(S_CH[:k]) for k in range(len(S_CH) + 1)]
         vm = [sm[-1] + sum(V_CH[:k]) for k in range(len(V_CH) + 1)]
         left = [sum(S_CH) + 2 * sum(V_CH)]
@@ -305,10 +307,10 @@ def rank_program(g, core, T, topo):
 
         def s_sub(k):
             a, n, bank = sm[k], 128 * S_CH[k], "ps%d" % (5 + k % 2)
-            mm(A(bank, 0, n), A("idn"), A("dd", 128 * a, 128 * a + n), True, False)
-            for c in range(0, n, 256):
-                d = min(c + 256, n)
-                mm(A(bank, c, d), A("nid"), A("yy", 0, d - c), False, d == n)
+            mm(A(bank, 0, n), A("idn"), A("dd", 128 * a, 128 * a + n), False, True)
+
+        def s_pre(k):
+            mm(A("ps%d" % (5 + k % 2), 0, 128 * S_CH[k]), A("nid"), A("yy", 0, 128 * S_CH[k]), True, False)
 
         def s_abs(k):
             act(A("rl", 128 * sm[k], 128 * sm[k + 1]), A("ps%d" % (5 + k % 2), 0, 128 * S_CH[k]), AF.Abs)
@@ -332,19 +334,24 @@ def rank_program(g, core, T, topo):
                 ev.append((ts_, 0, lambda k=k: s_gather(k)))
                 ts_ += 60 + 200 * S_CH[k]
                 ev.append((ts_, 1, lambda k=k: s_sub(k)))
+                if k < 2:
+                    ev.append((2 + k, 1, lambda k=k: s_pre(k)))
             else:
                 ev.append((ts_, 2, lambda k=k: s_abs(k)))
                 ts_ += 60 + 128 * S_CH[k]
-                ev.append((ts_ + LATE, 3, lambda k=k: keys("rl", sm[k], sm[k + 1], 8)))
+                if k + 2 < len(S_CH):
+                    ev.append((ts_, 0, lambda k=k: s_pre(k + 2)))
+                ev.append((ts_ + 1, 3, lambda k=k: keys("rl", sm[k], sm[k + 1], 8)))
         for w, k in turns(len(V_CH)):
             if w == "g":
                 ev.append((tv, 0, lambda k=k: v_gather(k)))
                 tv += 50 + 200 * V_CH[k]
-                ev.append((tv + LATE, 3, lambda k=k: keys("dd", vm[k], vm[k + 1], 24)))
+                ev.append((tv + (LATE if k < len(V_CH) - 2 else 0), 3, lambda k=k: keys("dd", vm[k], vm[k + 1], 24)))
             else:
                 ev.append((tv, 2, lambda k=k: v_relu(k)))
                 tv += 64 * V_CH[k]
-                ev.append((tv + LATE, 3, lambda k=k: keys("rl", vm[k], vm[k + 1], 16)))
+                ev.append((tv + (LATE if k < len(V_CH) - 2 else END if k == len(V_CH) - 1 else 0), 3,
+                           lambda k=k: keys("rl", vm[k], vm[k + 1], 16)))
         for e_ in sorted(ev, key=lambda x: x[:2]):
             e_[2]()
         scan(A("sk"), A("rk"), PK, OP.add, OP.min)
@@ -352,8 +359,7 @@ def rank_program(g, core, T, topo):
             act(col("aq", 0), PCNT, bias=R64)
             act(col("ar", 0), col("aq", 0), bias=R64, scale=-1.0)
             act(col("ac", 0), PCNT, bias=col("ar", 0))
-        copy(A("ki"), A("sk", 31, 256, 32))
-        ts(A("kj"), A("ki"), 255, OP.bitwise_and)
+        ts(A("kj"), A("sk", 31, 256, 32), 255, OP.bitwise_and)
         tt(A("ex"), ind(A("kj"), A("cexp")), A("dm", 0, 128), OP.mult)
         mm(PW, A("ex"), A("b8", 0, 8), True, True)
         mm(PN, A("idn"), A("half"), True, False)

@@ -2,46 +2,59 @@ import numpy as np
 from concourse.mybir import AluOpType as OP, ActivationFunctionType as AF
 
 W, L, M, RO, N = 4096, 128, 32, 5, 6
+XW = W + L
 BIG = float(1 << 22)
 R1 = float(3 << 22)
+R32 = float((1 << 28) + (1 << 23))
 R64 = float(3 << 28)
-V_LAG, LATE, END = 100, 200, 1000
-C_CUT = [0, 64, 128, 192, 256]
-Q_S = 2
-S_CH = [4, 4, 4, 2]
-V_CH = [2, 4, 4, 4, 3, 1]
-F, B16, I32, U16 = "float32", "bfloat16", "int32", "uint16"
+R128 = float(3 << 29)
+OFF = 2048.0
+CHUNKS = [[(_c[0], int(_c[1])) for _c in "S2 V1 S3 V1 V1 S3 V1 V1 S1 V1 V1".split()]] * 2
+NV_ON_S = False
+EX_ON_S = False
+CY, PCY, GA, SC, WAKE, HOLD = 0.9, 0.45, 1.25, 2.7, 215.0, 230.0
+YW = 128
+CLS, TOL, LOAD = 1000.0, 100.0, 4000.0
+F, B16, F16, I32, U16 = "float32", "bfloat16", "float16", "int32", "uint16"
 
 
 def _sb(cols, dt_):
     return ("sbuf", [128] + (cols if isinstance(cols, list) else [cols]), dt_)
 
 
-SCRATCH = {
-    "X": _sb(W + L, B16), "win": _sb(RO * 256, F), "h16": _sb(56, U16),
-    "rin": _sb(128, I32), "rf": _sb(256, F), "rt": _sb(256, F), "wti": _sb(4, I32), "kpi": _sb(4, I32),
-    "pc": _sb(16, I32), "pf": _sb(16, F), "pi": _sb(128, I32), "pj": _sb(128, I32), "j8": _sb(8, F),
-    "lt": _sb(8, U16), "cexp": _sb(8, U16), "jg": _sb(128, B16), "i8m": _sb(256, B16), "tg": _sb(128, B16),
-    "km": _sb(32, F), "kf": _sb(4, F), "wf": _sb(4, F),
-    "idn": _sb(128, B16), "nid": _sb(128, B16), "n128": _sb(128, B16), "dm": _sb(256, F), "nb": _sb(128, B16),
-    "bb": _sb(128, B16), "bf": _sb(128, F), "tri": _sb(128, B16), "wb": _sb(512, B16), "b8": _sb(32, B16),
-    "i4": _sb(64, F), "j4": _sb(64, B16), "nb4": _sb(64, B16), "rs4": _sb(64, F),
-    "rst": _sb(256, F), "rk": _sb(256, F), "d0": _sb(128, F), "ck": _sb(256, B16), "odd": _sb(32, F),
-    "kr": _sb(32, F), "fw": _sb(256, B16), "o16": _sb(128, F), "half": _sb(128, B16),
-    "xab": _sb(256, B16), "sa": _sb(64, I32), "aj": _sb(16, I32), "ao": _sb(16, U16),
-    "mpq": _sb(256, F), "spq": _sb(256, F), "opq": _sb(16, U16), "pqi": _sb(8, I32), "fi": _sb(8, I32),
-    "gg": _sb(8, F), "t1": _sb(256, F), "ci": _sb(256, I32), "cm": _sb(256, I32), "co": _sb(256, U16),
-    "junk": _sb(256, F), "cnt": _sb(4, F), "aq": _sb(4, F), "ar": _sb(4, F), "ac": _sb(4, F),
-    "xpq": _sb(256, B16), "sg": _sb(128, B16), "yy": _sb(512, B16),
-    "dd": _sb(W, B16), "rl": _sb(W, B16),
-    "sk": _sb(256, I32), "kj": _sb(8, I32), "ex": _sb(128, B16), "eo": _sb(8, U16),
-    "me": _sb(128, F), "se": _sb(128, F), "cmp": _sb([8, 128], B16), "sc": _sb(128, F), "so": _sb(8, U16),
-    "xe": _sb(128, B16), "uu": _sb(128, F), "nv": _sb(128, B16), "er": _sb(RO * 128, F),
+HALVES = {
+    "X": (XW, B16), "win": ((RO + 1) * 128, F), "h16": (32, U16), "wb": (512, B16),
+    "sel": (128, B16), "bsel": (128, B16),
+    "xab": (128, B16), "sa": (64, F), "ao": (8, U16), "cn": (8, B16),
+    "mpq": (128, F16), "spq": (256, F16), "opq": (8, U16), "pq": (8, F), "gg": (8, F), "tr": (32, F16),
+    "ci": (128, I32), "cm": (128, I32), "cf": (128, F), "co": (128, U16), "xpq": (128, B16), "yy": (256, B16),
+    "dd": (W // 2, B16), "rl": (W // 2, B16), "sk": (256, I32), "ex": (128, B16), "kj": (8, I32),
+    "eo": (8, U16), "me": (64, F16), "se": (64, F), "sc": (128, F), "so": (8, U16), "xe": (64, B16),
+    "uu": (128, F), "nv": (128, B16), "ni": (128, I32), "ry": (128, F),
 }
+SCRATCH = {_n: _sb(2 * _v[0], _v[1]) for _n, _v in HALVES.items()}
+SCRATCH.update({
+    "cmp": _sb([8, 128], B16), "R": _sb([2, 4, 32], F16), "mc": _sb(192, B16),
+    "rin": _sb(128, I32), "r16": _sb(128, F16), "wti": _sb(4, I32), "kpi": _sb(4, I32), "kpj": _sb(4, I32),
+    "pc": _sb(8, I32), "pf": _sb(16, F), "j8": _sb(8, F), "jp": _sb(128, B16), "jg": _sb(128, B16),
+    "jq": _sb(128, B16), "jc": _sb(128, B16), "j16": _sb(128, B16), "i8": _sb(64, F), "j4": _sb(64, F),
+    "i4m": _sb(256, B16), "odd": _sb(64, F), "w4": _sb(8, B16), "wf": _sb(4, F), "kf": _sb(8, F), "km": _sb(64, F16),
+    "pk": _sb(8, F), "sl": _sb(8, F), "cs": _sb(8, F), "c1": _sb(64, F), "c2": _sb(64, F), "g0": _sb(128, B16),
+    "g1": _sb(128, B16), "g2": _sb(128, B16),
+    "idn": _sb([2, 4, 16], B16), "nid": _sb(128, B16), "idf": _sb(128, F), "dm": _sb(128, B16),
+    "nb": _sb(128, B16), "bb": _sb(128, B16), "qq": _sb(128, B16), "qc": _sb(256, B16), "qs": _sb(256, B16),
+    "tri": _sb(256, B16), "b8": _sb(32, B16), "ca": _sb(128, B16), "rs8": _sb(64, F),
+    "rst": _sb(128, B16), "rk": _sb(256, F), "d0": _sb(128, F), "ck": _sb(256, B16), "cexp": _sb(8, U16),
+    "one": _sb(128, B16), "half": _sb(128, B16),
+    "junk": _sb(16, F), "cnt": _sb(4, F), "aq": _sb(4, F), "ar": _sb(4, F), "ac": _sb(4, F),
+})
 for _k in range(8):
     SCRATCH["ps%d" % _k] = ("psum", [128, 512], F)
 
-SEMAPHORES = ["cV", "cS", "cP", "cG", "sent"] + ["arr%d" % _t for _t in range(RO)] + ["dq%d" % _k for _k in range(24)]
+SEMAPHORES = (["cV", "cS", "cP", "cG", "sent"] + ["arr%d" % _t for _t in range(2 * RO)]
+              + ["ldx0", "ldx1", "out"] + ["dq%d" % _k for _k in range(16)])
+COLS = {}
+PLAN = {}
 
 
 def rank_program(g, core, T, topo):
@@ -50,16 +63,16 @@ def rank_program(g, core, T, topo):
         return
     ops = []
     ALL = slice(None)
+    st = {"cls": 1}
 
-    def cols(a):
-        name, idx = a[0], a[1]
-        shape = SCRATCH[name][1][1:]
-        m = np.zeros(shape, bool)
-        m[idx[1:]] = True
-        return m.reshape(-1)
+    def A(name, lo=None, hi=None, step=None, part=ALL):
+        return (name, (part, slice(lo, hi, step)))
 
-    def A(name, lo=None, hi=None, step=None):
-        return (name, (ALL, slice(lo, hi, step)))
+    def half(H):
+        def a(name, lo=0, hi=None, step=None, part=ALL):
+            n = HALVES[name][0]
+            return (name, (part, slice(H * n + lo, H * n + (n if hi is None else hi), step)))
+        return a
 
     def ind(win, off):
         return (win[0], win[1], off)
@@ -70,348 +83,472 @@ def rank_program(g, core, T, topo):
         v = T[a[0]][a[1]]
         return v.indirect(ap(a[2])) if len(a) == 3 else v
 
-    def add(eng, call, outs, ins, dma=False, after=(), waits=()):
-        rd, wr = [], []
-        for a in ins:
-            if isinstance(a, tuple):
-                rd.append((a[0], cols(a)))
-                if len(a) == 3:
-                    rd.append((a[2][0], cols(a[2])))
-        for a in outs:
-            wr.append((a[0], cols(a)))
-            if len(a) == 3:
-                rd.append((a[2][0], cols(a[2])))
-        ops.append({"eng": eng, "call": call, "rd": rd, "wr": wr, "dma": dma, "after": list(after), "waits": list(waits)})
+    def add(eng, kind, call, outs, ins, **kw):
+        o = {"eng": eng, "kind": kind, "call": call, "outs": outs, "ins": [a for a in ins if isinstance(a, tuple)],
+             "dma": False, "after": [], "soft": [], "waits": [], "acc": None, "stop": False, "cls": st["cls"], "sem": None}
+        o.update(kw)
+        ops.append(o)
         return len(ops) - 1
 
     V, S, P = g.vector, g.scalar, g.tensor
 
     def copy(o, i):
-        return add("V", lambda: V.tensor_copy(ap(o), ap(i)), [o], [i])
+        return add("V", "c", lambda _o: V.tensor_copy(ap(o), ap(i)), [o], [i])
 
-    def tt(o, a, b, op, waits=()):
-        return add("V", lambda: V.tensor_tensor(ap(o), ap(a), ap(b), op), [o], [a, b], waits=waits)
+    def tt(o, a, b, op, **kw):
+        return add("V", "tt", lambda _o: V.tensor_tensor(ap(o), ap(a), ap(b), op), [o], [a, b], **kw)
 
     def ts(o, a, s1, op0, s2=None, op1=None):
         if op1 is None:
-            return add("V", lambda: V.tensor_scalar(ap(o), ap(a), ap(s1), None, op0), [o], [a, s1])
-        return add("V", lambda: V.tensor_scalar(ap(o), ap(a), ap(s1), ap(s2), op0, op1), [o], [a, s1, s2])
+            return add("V", "c", lambda _o: V.tensor_scalar(ap(o), ap(a), ap(s1), None, op0), [o], [a, s1])
+        return add("V", "c", lambda _o: V.tensor_scalar(ap(o), ap(a), ap(s1), ap(s2), op0, op1), [o], [a, s1, s2])
 
     def scan(o, d0, d1, op0, op1):
-        return add("V", lambda: V.tensor_tensor_scan(ap(o), ap(d0), ap(d1), 0.0, op0, op1), [o], [d0, d1])
+        return add("V", "c", lambda _o: V.tensor_tensor_scan(ap(o), ap(d0), ap(d1), 0.0, op0, op1), [o], [d1, d0])
 
     def fill(o, c):
-        return add("V", lambda: V.memset(ap(o), c), [o], [])
+        return add("V", "c", lambda _o: V.memset(ap(o), c), [o], [])
 
     def act(o, i, f=AF.Identity, bias=0.0, scale=1.0, acc=None):
         if acc is None:
-            return add("S", lambda: S.activation(ap(o), ap(i), f, bias=ap(bias), scale=ap(scale)), [o], [i, bias, scale])
-        return add("S", lambda: S.activation(ap(o), ap(i), f, bias=ap(bias), scale=ap(scale), accum_out=ap(acc)),
+            return add("S", "a", lambda _o: S.activation(ap(o), ap(i), f, bias=ap(bias), scale=ap(scale)), [o], [i, bias, scale])
+        return add("S", "a", lambda _o: S.activation(ap(o), ap(i), f, bias=ap(bias), scale=ap(scale), accum_out=ap(acc)),
                    [o, acc], [i, bias, scale])
 
-    def mm(o, l, r, start, stop):
-        return add("P", lambda: P.matmul(ap(o), ap(l), ap(r), start, stop), [o], [l, r])
+    def mm(o, l, r, start, stop, acc=None):
+        return add("P", "m", lambda _o: P.matmul(ap(o), ap(l), ap(r), start, _o["stop"]), [o], [l, r], acc=acc, stop=stop)
 
     def iota(o, pat, base, cm):
         if SCRATCH[o[0]][2] == I32:
-            return add("G", lambda: g.iota(ap(o), pat, base, cm), [o], [])
-        return add("G", lambda: g.iota(ap(o), pat, base, cm, allow_small_or_imprecise_dtypes=True), [o], [])
+            return add("G", "g", lambda _o: g.iota(ap(o), pat, base, cm), [o], [])
+        return add("G", "g", lambda _o: g.iota(ap(o), pat, base, cm, allow_small_or_imprecise_dtypes=True), [o], [])
 
-    def dma(q, o, i, after=()):
+    def dma(q, o, i, sem=None):
         Q = {"Y": g.sync, "S": g.scalar}[q]
-        return add(q, lambda: Q.dma_start(ap(o), ap(i)), [o] if isinstance(o, tuple) else [], [i], dma=True, after=after)
+        return add(q, "d", lambda _o: Q.dma_start(ap(o), ap(i)), [o] if isinstance(o, tuple) else [], [i], dma=True, sem=sem)
 
-    sent = [0]
+    sent, sends = [0], {}
 
-    def engines(src, dst, kind):
-        es = topo.engines(src, dst)
-        return (es[0::2], es[1::2], es)[kind]
-
-    def send(kind, t, dst, src, after=()):
+    def send(H, t):
+        a = half(H)
         peer = T.cores[(rank - 1 - t) % N]
         rid, pid, _se = topo.addr(peer)
-        es = engines(core, peer, kind)
-        mask = sum(1 << e for e in es)
-        sent[0] += len(es)
-        add("G", lambda: g.remote_dma(ap(dst), ap(src), T.sem["arr%d" % t], T.sem.sent, pid, rid, mask), [], [src],
-            dma="remote", after=after)
+        sent[0] += len(topo.engines(core, peer))
+        src, dst = a("win", 128 * t, 128 * t + 64), a("win", 128 * t + 64, 128 * t + 128)
+        sends[H, t] = add("G", "r", lambda _o: g.remote_dma(ap(dst), ap(src), T.sem["arr%d" % (2 * t + H)], T.sem.sent, pid, rid,
+                                                            topo.mask(core, peer)), [], [src], dma="remote")
 
-    def arrivals(t):
-        return sum(len(engines(T.cores[(rank + 1 + t) % N], core, kind)) for kind in ((0,) if t == 0 else (1, 2)))
+    def arrival(H, t):
+        return ("arr%d" % (2 * t + H), len(topo.engines(T.cores[(rank + 1 + t) % N], core)))
 
     col = lambda name, j: A(name, j, j + 1)
-    XW = A("X", 0, W)
+    IDN = ("idn", (ALL, ALL, ALL, ALL))
+    quad = lambda q: slice(32 * q, 32 * q + 32)
+    lanes = lambda bank, b0, b1: A(bank, 32 * b0, 32 * b1)
+    copy_c = lambda bank, c: A(bank, c, 128, 2)
+
+    def load_x(H):
+        for q in range(4):
+            for c in range(2):
+                p0, r0 = 32 * q + 16 * c, 16 * (4 * H + q)
+                dma("YS"[c], half(H)("X", 0, W, part=slice(p0, p0 + 16)), T.x[r0:r0 + 16, :], sem="ldx%d" % H)
 
     dma("Y", A("rin"), T.ring[:])
-    dma("Y", XW, T.x[:])
-    dma("S", A("kpi", 0, 2), T.kap[:])
     dma("S", A("wti", 0, 1), T.wt[:])
+    load_x(0)
+    dma("S", A("kpi", 0, 2), T.kap[:])
+    load_x(1)
 
     iota(col("pc", 0), [[0, 1]], 0, 1)
-    iota(A("j8"), [[1, 8]], 0, 0)
-    iota(A("pi"), [[1, 128]], 0, -1)
+    iota(A("jp"), [[1, 128]], 0, 0)
+    iota(A("jc"), [[16, 4], [0, 2], [1, 16]], 0, 0)
     iota(A("jg"), [[1, 8], [0, 16]], 0, 0)
-    iota(A("i4"), [[0, 16], [1, 4]], 0, 0)
-    iota(A("j4"), [[0, 2], [1, 8], [0, 4]], 0, 0)
-    iota(A("odd"), [[2, 32]], 1, 0)
-    iota(A("i8m"), [[0, 8], [8, 32]], 0, 0)
+    iota(A("j16"), [[0, 8], [1, 16]], 0, 0)
+    iota(A("jq"), [[1, 4], [0, 32]], 0, 0)
+    iota(A("j8"), [[1, 8]], 0, 0)
+    iota(A("i8"), [[0, 8], [1, 8]], 0, 0)
+    iota(A("j4"), [[0, 2], [1, 4], [0, 8]], 0, 0)
+    iota(A("odd"), [[0, 2], [2, 32]], 65, 0)
+    iota(A("i4m"), [[0, 8], [4, 32]], 0, 0)
+    ts(col("pc", 1), col("pc", 0), 4, OP.arith_shift_right)
+    ts(col("pc", 2), col("pc", 0), 15, OP.bitwise_and)
+    ts(col("pc", 3), col("pc", 0), 5, OP.arith_shift_right)
+    ts(col("pc", 4), col("pc", 0), 4, OP.arith_shift_right, 1, OP.bitwise_and)
+    ts(col("pc", 5), col("pc", 0), 1, OP.arith_shift_right, 7, OP.bitwise_and)
+    ts(col("pc", 6), col("pc", 0), 3, OP.arith_shift_right, 3, OP.bitwise_and)
+    ts(col("pc", 7), col("pc", 0), 7, OP.bitwise_and)
+    copy(col("pf", 0), col("pc", 0))
+    copy(A("pf", 1, 8), A("pc", 1, 8))
+    p_, pg_, r_, q_, hi_, kind_, s7_ = [col("pf", j) for j in (0, 1, 2, 3, 5, 6, 7)]
+    ts(IDN, A("jp"), p_, OP.is_equal)
     fill(A("half"), -0.5)
-    fill(A("X", W, W + L), 0.0)
-    act(A("fw", 0, 128), A("half"), scale=0.0)
-    act(A("fw", 128, 256), A("half"), scale=-2.0)
-    act(A("o16"), A("half"), scale=-0.125)
-    act(A("rk", 0, 128), A("half"), scale=0.0)
-    act(A("rk", 128, 256), A("half"), scale=0.0)
-    act(A("d0"), A("half"), scale=0.0)
-    act(A("rk", 0, 256, 32), A("half", 0, 8), scale=-2.0 * BIG)
-    ts(col("pc", 1), col("pc", 0), 4, OP.arith_shift_right, 1, OP.bitwise_and)
-    ts(col("pc", 2), col("pc", 0), 3, OP.arith_shift_right, 1, OP.bitwise_and)
-    ts(col("pc", 3), col("pc", 0), 4, OP.arith_shift_right)
-    ts(col("pc", 4), col("pc", 0), 15, OP.bitwise_and)
-    ts(col("pc", 5), col("pc", 0), 2, OP.arith_shift_right, 3, OP.bitwise_and)
-    tt(col("pc", 8), col("pc", 0), col("pc", 1), OP.subtract)
-    copy(A("pf", 0, 6), A("pc", 0, 6))
-    ts(col("pc", 6), col("pc", 8), 7, OP.bitwise_and)
-    ts(col("pc", 7), col("pc", 8), 1, OP.bitwise_and)
-    copy(A("cexp"), A("j8"))
-    ts(col("pf", 6), col("pc", 6), col("pf", 1), OP.add, 16.0, OP.mult)
-    ts(col("pf", 7), col("pc", 7), 112.0, OP.mult, col("pf", 2), OP.add)
-    ts(A("pj"), A("pi"), 15, OP.bitwise_and)
-    tt(col("pf", 8), col("pf", 6), col("pf", 7), OP.add)
-    ts(A("idn"), A("pi"), 0.0, OP.is_equal)
-    ts(A("lt"), A("j8"), 2.0, OP.mult, col("pf", 8), OP.add)
-    ts(A("bb"), A("jg", 0, 128), col("pf", 3), OP.is_equal)
-    ts(A("dm", 0, 128), A("pj"), 0.0, OP.is_equal)
-    fill(A("wb"), 0.0)
-    ts(A("nb4"), A("i4"), col("pf", 5), OP.not_equal, -BIG, OP.mult)
-    ts(A("rs4"), A("i4"), 1.0, OP.min)
-    copy(A("rf", 0, 128), A("rin"))
-    copy(A("rf", 128, 240), A("rin", 16, 128))
-    copy(A("rf", 240, 256), A("rin", 0, 16))
-    add("V", lambda: V.transpose(ap(A("rt")), ap(A("rf"))), [A("rt")], [A("rf")])
-    ts(col("wf", 0), col("wti", 0), 8.0, OP.mult)
-    copy(A("win", 0, 128), ind(A("rt"), A("lt")))
-    send(0, 0, A("win", 128, 256), A("win", 0, 128))
-    copy(A("kf", 0, 2), A("kpi", 0, 2))
-    copy(A("h16", 40, 56), A("win", 0, 16))
-    act(A("bf"), A("bb"))
-    act(A("dm", 128, 256), A("dm", 0, 128))
-    act(A("nb"), A("dm", 0, 128), bias=-BIG, scale=BIG)
-    act(A("nid"), A("idn"), scale=-1.0)
-    act(A("n128"), A("idn"), scale=-128.0)
+    fill(A("one"), 1.0)
+    ts(A("r16"), A("rin"), -OFF, OP.add)
     for q in range(4):
-        act(A("wb", 129 * q, 128 * q + 128, 4), A("bb", q, 128, 4), scale=col("wf", 0))
-    ts(A("km", 0, 16), A("dm", 0, 16), col("kf", 0), OP.mult)
-    ts(A("km", 16, 32), A("dm", 0, 16), col("kf", 1), OP.mult)
-    fill(A("rst"), 1.0)
-    add("G", lambda: g.affine_select(ap(A("tri")), ap(A("bb")), [[1, 128]], OP.is_gt, 0.0, 0, -1), [A("tri")], [A("bb")])
-    mm(A("ps7", 0, 32), A("bf"), A("km"), True, True)
-    PA = A("ps0", 0, 64)
-
-    def age_const():
-        mm(PA, A("idn"), A("nb4"), True, False)
-        mm(PA, A("idn"), A("j4"), False, False)
-
-    age_const()
-    act(A("b8", 0, 8), A("bb", 0, 128, 16))
-    act(A("b8", 8, 16), A("bb", 0, 128, 16), scale=256.0)
-    act(A("b8", 16, 24), A("bb", 0, 128, 16), scale=512.0)
-    act(A("b8", 24, 32), A("bb", 0, 128, 16), scale=-256.0)
-    act(A("kr"), A("ps7", 0, 32))
-    ts(col("pf", 9), col("pf", 4), float(W), OP.add)
-    ts(A("ck"), A("i8m"), col("pf", 3), OP.add)
-    fill(A("rst", 0, 256, 16), 0.0)
-    ts(A("d0", 0, 128, 16), A("j8"), 16.0, OP.mult, col("pf", 9), OP.add)
-
-    PT, PC, PK = A("ps1", 0, 256), A("ps1", 0, 128), A("ps2", 0, 256)
-    PY1, PW, PY2, PE_ = A("ps3", 0, 128), A("ps3", 0, 8), A("ps4", 0, 256), A("ps4", 0, 128)
-    PN, PCNT = A("ps7", 0, 128), A("ps7", 0, 1)
-    diag = lambda name, n: A(name, 15, n, 16)
-
-    for t in range(RO):
-        last = t == RO - 1
-        w0 = 256 * t
-        h0 = 8 * (RO - t)
-        copy(A("xab", 0, 128), ind(XW, A("h16", h0, h0 + 8)))
-        act(A("xab", 128, 256), ind(XW, A("h16", h0 + 8, h0 + 16)))
-        for q in range(4):
-            mm(PA, A("wb", 128 * q, 128 * q + 128), A("xab", q, 256, 4), False, q == 3)
-        scan(A("sa"), A("rs4"), PA, OP.mult, OP.max)
-        ts(A("aj"), A("sa", 3, 64, 4), 255, OP.bitwise_and)
-        copy(A("ao"), A("aj"))
-        tt(A("mpq", 0, 128), ind(A("win", w0, w0 + 256), A("ao", 0, 8)), A("dm", 0, 128), OP.mult,
-           waits=[("arr%d" % t, arrivals(t))])
-        tt(A("mpq", 128, 256), ind(A("win", w0, w0 + 256), A("ao", 8, 16)), A("dm", 0, 128), OP.mult)
-        if not last:
-            act(A("junk"), ind(A("fw"), A("ao")), bias=-63.0 / 4096, acc=col("cnt", 0))
-        Pc = lambda ii: col("spq", 16 * ii + 15)
-        Qc = lambda ii: col("spq", 128 + 16 * ii + 15)
-        kp = lambda ii: ts(A("ps1", ii, 256, 8), A("kr"), Pc(ii), OP.mult)
-        scan(A("spq", 0, 128), A("rst", 0, 128), A("mpq", 0, 128), OP.mult, OP.max)
-        spq = scan(A("spq", 128, 256), A("rst", 0, 128), A("mpq", 128, 256), OP.mult, OP.max)
-        kp(0)
-        copy(A("opq", 0, 8), diag("spq", 128))
-        act(A("xpq", 0, 128), ind(XW, A("opq", 0, 8)))
-        kp(1)
-        if t == 0:
-            old = dma("Y", T.yr[RO:128, :], ("rf", (slice(0, 128 - RO), slice(0, 128))), after=[spq])
-        if not last:
-            mm(PCNT, A("o16"), col("cnt", 0), True, True)
-            dma("Y", A("win", w0 + 264, w0 + 384), A("win", w0, w0 + 120), after=[spq])
-            send(1, t + 1, A("win", w0 + 256 + 136, w0 + 512), A("win", w0, w0 + 120), after=[spq])
-        copy(A("opq", 8, 16), A("spq", 143, 256, 16))
-        tt(A("pqi"), A("spq", 15, 128, 16), A("spq", 143, 256, 16), OP.mult)
-        act(A("xpq", 128, 256), ind(XW, A("opq", 8, 16)))
-        for ii in (2, 3, 4):
-            kp(ii)
-        ts(A("fi"), A("pqi"), 5, OP.arith_shift_right)
-        for ii in (5, 6, 7):
-            kp(ii)
-        if t == 0:
-            copy(A("gg"), A("fi"))
-        else:
-            ts(A("gg"), A("fi"), col("ac", 0), OP.add, 31.5, OP.add)
-        mm(PY1, A("idn"), A("xpq", 0, 128), True, False)
-        mm(PY1, A("idn"), A("xpq", 128, 256), False, True)
-        mm(PY2, A("idn"), A("xpq"), True, False)
-        mm(A("ps4", 0, 128), A("idn"), A("xpq", 128, 256), False, False)
-        mm(A("ps4", 128, 256), A("idn"), A("xpq", 0, 128), False, False)
-        for ii in range(Q_S):
-            act(A("t1", ii, 256, 8), A("odd"), scale=Qc(ii), bias=col("gg", ii))
-        act(A("sg"), PY1, AF.Sign, bias=-255.5)
+        for ib in range(4):
+            mm(A("ps7", ib, 128, 4, part=quad(q)), A("r16", 32 * ib, 32 * ib + 32), ("idn", (ALL, ALL, q, ALL)), True, True)
+    for H in range(2):
+        act(half(H)("win", 0, 64), A("ps7", 64 * H, 64 * H + 64))
+        send(H, 0)
+        ts(half(H)("h16", 4 * RO, 4 * RO + 8), half(H)("win", 0, 8), OFF, OP.add)
+    ts(col("pf", 8), p_, -64.0, OP.add)
+    ts(col("pf", 9), pg_, -4.0, OP.add)
+    ts(col("w4", 0), col("wti", 0), 4.0, OP.mult)
+    ts(A("bb"), A("jg"), pg_, OP.is_equal)
+    ts(A("dm"), A("j16"), r_, OP.is_equal)
+    fill(A("wb"), 0.0)
+    for H in range(2):
+        ts(half(H)("sel"), A("jc"), (p_, col("pf", 8))[H], OP.is_equal)
+        ts(half(H)("bsel"), A("jq"), (pg_, col("pf", 9))[H], OP.is_equal)
+        mm(col("ps4", H), half(H)("sel"), col("w4", 0), True, True)
+    act(A("wf", 0, 2), A("ps4", 0, 2))
+    act(A("wf", 2, 4), A("ps4", 0, 2), scale=-1.0)
+    for H in range(2):
+        for k in range(4):
+            act(half(H)("wb", 128 * k + k % 2, 128 * k + 128, 2), A("bb", k % 2, 128, 2), scale=col("wf", H + 2 * (k // 2)))
+    ts(A("c1"), A("i8"), hi_, OP.not_equal, -BIG, OP.mult)
+    tt(A("ca", 64, 128), A("c1"), A("j4"), OP.add)
+    ts(A("ca", 0, 64), A("j4"), -1.0, OP.mult, 63.5, OP.add)
+    ts(A("rs8"), A("i8"), 1.0, OP.min)
+    for k, c in enumerate((R128, 2 * R128, 127.5)):
+        act(A("mc", 64 * k, 64 * k + 64), A("one", 0, 64), scale=c)
+    act(A("rst"), A("one"))
+    act(A("rst", 0, 128, 16), A("one", 0, 8), scale=0.0)
+    ts(A("kpj", 0, 2), A("kpi", 0, 2), 1, OP.bitwise_and)
+    ts(A("kf", 0, 2), A("kpi", 0, 2), 1984.0, OP.is_gt, -4096.0, OP.mult)
+    ts(A("kf", 2, 4), A("kpi", 0, 2), 64.0, OP.add)
+    tt(A("kf", 4, 6), A("kf", 0, 2), A("kf", 2, 4), OP.add)
+    ts(A("kf", 6, 8), A("kpj", 0, 2), OFF, OP.mult, 31.0 - OFF, OP.add)
+    for k in range(4):
+        ts(A("km", 16 * k, 16 * k + 16), A("dm", 0, 16), col("kf", 4 + k), OP.mult)
+    for H in range(2):
         for k in range(2):
-            mm(A("ps4", 128 * k, 128 * k + 128), A("n128"), A("sg"), False, k == 1)
-        for ii in range(Q_S, 8):
-            ts(A("t1", ii, 256, 8), A("odd"), Qc(ii), OP.mult, col("gg", ii), OP.add)
-        act(A("yy", 0, 256), PY2, bias=-128.0)
-        mm(PK, A("idn"), A("ck"), True, False)
-        parts = list(zip(C_CUT[:-1], C_CUT[1:]))
-        for a, b in parts:
-            tt(A("ci", a, b), A("t1", a, b), A("ps1", a, b), OP.add)
-        for a, b in parts:
-            ts(A("cm", a, b), A("ci", a, b), W - 1, OP.bitwise_and)
-        for a, b in parts:
-            copy(A("co", a, b), A("cm", a, b))
-        copy(A("yy", 256, 512), A("yy", 0, 256))
-        sm = [sum(S_CH[:k]) for k in range(len(S_CH) + 1)]
-        vm = [sm[-1] + sum(V_CH[:k]) for k in range(len(V_CH) + 1)]
-        left = [sum(S_CH) + 2 * sum(V_CH)]
+            mm(lanes("ps5", 2 * k + H, 2 * k + H + 1), half(H)("bsel"), A("km", 32 * k, 32 * k + 32), True, True)
+    ts(A("pk"), A("j8"), kind_, OP.is_equal)
+    ts(A("sl"), A("j8"), s7_, OP.is_equal)
+    ts(A("cs"), A("j8"), col("pf", 4), OP.is_equal)
+    act(A("odd"), A("odd"), scale=col("pk", 1))
+    act(A("c1"), lanes("ps5", 0, 2), scale=col("pk", 0))
+    act(A("c2"), lanes("ps5", 2, 4), scale=col("pk", 2))
+    tt(A("c1"), A("c1"), A("c2"), OP.add)
+    tt(A("c2"), A("c1"), A("odd"), OP.add)
+    for ib in range(4):
+        ts(("R", (ALL, ALL, ib, ALL)), A("c2"), col("sl", 2 * ib + 1), OP.mult)
+    fill(A("sk"), 0)
+    for H in range(2):
+        copy(half(H)("spq", 128, 256), A("one"))
+        fill(half(H)("X", W, XW), 0.0)
+    act(A("nid"), IDN, scale=-1.0)
+    act(A("idf"), IDN)
+    for c in range(2):
+        act(copy_c("nb", c), A("dm", 0, 64), bias=BIG, scale=-BIG)
+    for k, s in enumerate((128.0, 256.0, -128.0, 1.0)):
+        act(A("b8", 8 * k, 8 * k + 8), A("bb", 0, 128, 16), scale=s)
+    ts(A("ck"), A("i4m"), pg_, OP.add)
+    fill(A("rk"), 0.0)
+    act(A("rk", 0, 256, 32), A("one", 0, 8), scale=BIG)
+    act(A("d0"), A("one"), scale=-2 * OFF)
+    ts(col("pf", 10), r_, W - OFF, OP.add)
+    ts(A("d0", 0, 128, 16), A("j8"), 16.0, OP.mult, col("pf", 10), OP.add)
+    copy(A("cexp"), A("j8"))
+    ts(A("qq"), A("jq"), q_, OP.is_equal)
+    ts(col("pf", 11), q_, 16.0, OP.mult, r_, OP.add)
+    ts(col("pf", 12), q_, 16.0, OP.mult, 15.0, OP.add)
+    ts(col("pf", 13), col("cs", 1), 99.0, OP.mult, col("pf", 11), OP.add)
+    ts(col("pf", 14), q_, 16.0, OP.mult, -1.0, OP.add)
+    ts(col("pf", 15), r_, 1.0, OP.add, col("cs", 1), OP.mult)
+    tt(col("pf", 14), col("pf", 14), col("pf", 15), OP.add)
+    for c in range(2):
+        act(A("qc", 128 * c, 128 * c + 128), A("qq"), scale=col("cs", c))
+        ts(A("qs", 128 * c, 128 * c + 128), A("jc"), col("pf", 11), OP.is_equal, col("cs", c), OP.mult)
+    ts(A("g0"), A("jc"), col("pf", 13), OP.is_gt)
+    ts(A("g1"), A("jc"), col("pf", 14), OP.is_gt)
+    tt(A("tri", 0, 128), A("g0"), A("qq"), OP.mult)
+    tt(A("tri", 128, 256), A("g1"), A("qq"), OP.mult)
 
-        def keys(buf, m0, m1, c):
-            for m in range(m0, m1):
-                left[0] -= 1
-                mm(A("ps2", m, 256, 32), A(buf, 128 * m, 128 * m + 128), A("b8", c, c + 8), False, left[0] == 0)
+    sbank = [0]
 
-        def s_gather(k):
-            act(A("dd", 128 * sm[k], 128 * sm[k + 1]), ind(XW, A("co", 8 * sm[k], 8 * sm[k + 1])))
+    def pre(H, t):
+        a = half(H)
+        st["cls"] = 1
+        X, w0, h0 = a("X", 0, W), 128 * t, 4 * (RO - t)
+        own = "ps%d" % (2 + H)
+        PA, PY, PS = A(own, 0, 64), A("ps6", 0, 64), lambda *s, **k: A("ps7", *s, **k)
+        dma("Y", a("win", w0 + 132, w0 + 192), a("win", w0, w0 + 60), sem="dq%d" % (3 + 2 * t + H))
+        act(a("xab"), ind(X, a("h16", h0, h0 + 8)))
+        mm(PA, IDN, A("ca", 0, 64), True, False)
+        for k in (2, 3):
+            mm(PA, a("wb", 128 * k, 128 * k + 128), a("xab", k % 2, 128, 2), False, False)
+        mm(PA, IDN, A("mc", 0, 64), False, False)
+        mm(PA, A("nid"), A("mc", 0, 64), False, False)
+        for k in (0, 1):
+            mm(PA, a("wb", 128 * k, 128 * k + 128), a("xab", k % 2, 128, 2), False, False)
+        mm(PA, IDN, A("ca", 64, 128), False, True)
+        scan(a("sa"), A("rs8"), PA, OP.mult, OP.max)
+        copy(a("ao"), a("sa", 7, 64, 8))
+        tt(a("mpq"), ind(a("win", w0, w0 + 128), a("ao")), A("dm"), OP.mult, waits=[arrival(H, t)], after=[sends[H, t]])
+        scan(a("spq", 0, 128), A("rst"), a("mpq"), OP.mult, OP.add)
+        add("V", "c", lambda _o: V.transpose(ap(a("tr")), ap(a("spq", 7, 256, 8))), [a("tr")], [a("spq", 7, 256, 8)])
+        tt(a("pq", 0, 4), a("spq", 15, 64, 16), a("spq", 79, 128, 16), OP.mult)
+        ts(a("opq"), a("spq", 15, 128, 16), OFF, OP.add)
+        for k, bank in enumerate(("ps7", own)):
+            for q in range(4):
+                mm(A(bank, 0, 64, part=quad(q)), a("tr", part=quad(q)), ("R", (quad(q), H, slice(2 * k, 2 * k + 2), ALL)), True, True)
+        ts(a("gg", 0, 4), a("pq", 0, 4), -1007.5 if t == 0 else col("ac", t % 2), OP.add, R32, OP.add)
+        act(a("xpq"), ind(X, a("opq")))
+        mm(PY, IDN, A("mc", 128, 192), True, False)
+        for k, l in enumerate((A("nid"), IDN)):
+            mm(PY, l, a("xpq", 0, 64), False, False)
+            mm(PY, l, a("xpq", 64, 128), False, k == 1)
+            if k == 0:
+                mm(PY, IDN, A("mc", 64, 128), False, False)
+                mm(PY, A("nid"), A("mc", 64, 128), False, False)
+        for ib in range(4):
+            ts(a("ci", ib, 128, 4), lanes(("ps7", own)[ib // 2], ib % 2, ib % 2 + 1), 32.0, OP.mult, a("gg", ib, ib + 1), OP.add)
+        for k in range(2):
+            ts(a("cm", 64 * k, 64 * k + 64), a("ci", 64 * k, 64 * k + 64), 5, OP.arith_shift_right, W - 1, OP.bitwise_and)
+        for k in range(2):
+            copy(a("co", 64 * k, 64 * k + 64), a("cm", 64 * k, 64 * k + 64))
+        for k in range(YW // 64):
+            act(a("yy", 64 * k, 64 * k + 64), PY)
+        st["cls"] = 0
+        ts(a("cf"), a("cm"), -OFF, OP.add)
+        if t < RO - 1:
+            ts(a("cn"), a("sa", 7, 64, 8), 64.0, OP.is_ge)
+            mm(PS(256 + 8 * H, 264 + 8 * H), A("one"), a("cn"), True, True)
+            if H == 1:
+                act(A("junk"), PS(256, 272), bias=-(31 + 15.5 / 32) / 16, acc=col("cnt", 0))
+                act(col("aq", 0), col("cnt", 0), bias=R64)
+                act(col("ar", 0), col("aq", 0), bias=32 * R64, scale=-32.0)
+                act(col("ac", (t + 1) % 2), col("cnt", 0), bias=col("ar", 0), scale=32.0)
 
-        def s_sub(k):
-            a, n, bank = sm[k], 128 * S_CH[k], "ps%d" % (5 + k % 2)
-            mm(A(bank, 0, n), A("idn"), A("dd", 128 * a, 128 * a + n), False, True)
+    def score(H, t):
+        a = half(H)
+        X, bank, grp = a("X", 0, W), "ps%d" % (2 + H), (H, t)
+        st["cls"] = 1
+        low = slice(0, 64)
+        mm(A(bank, 0, 256, part=low), ("idn", (ALL, 0, ALL, ALL)), A("ck"), True, False)
+        st["cls"] = 0
+        line = {}
 
-        def s_pre(k):
-            mm(A("ps%d" % (5 + k % 2), 0, 128 * S_CH[k]), A("nid"), A("yy", 0, 128 * S_CH[k]), True, False)
+        def turn(who, n):
+            if who in line:
+                ops[n]["soft"].append(line[who])
+            line[who] = n
 
-        def s_abs(k):
-            act(A("rl", 128 * sm[k], 128 * sm[k + 1]), A("ps%d" % (5 + k % 2), 0, 128 * S_CH[k]), AF.Abs)
+        def keys(buf, p0, n, c):
+            for m in range(2 * p0, 2 * (p0 + n)):
+                mm(A(bank, m, 256, 32, part=low), a(buf, 64 * m, 64 * m + 64), A("b8", c, c + 8), False, False, acc=grp)
 
-        def v_gather(k):
-            a, b = vm[k], vm[k + 1]
-            tt(A("dd", 128 * a, 128 * b), ind(XW, A("co", 8 * a, 8 * b)), A("yy", 0, 128 * (b - a)), OP.subtract)
-
-        def v_relu(k):
-            ts(A("rl", 128 * vm[k], 128 * vm[k + 1]), A("dd", 128 * vm[k], 128 * vm[k + 1]), 0.0, OP.max)
-
-        def consts():
-            mm(PC, A("nid"), A("nb"), True, False)
-            if not last:
-                age_const()
-
-        turns = lambda n: [("g", 0)] + sum([[("g", k + 1), ("a", k)] for k in range(n - 1)], []) + [("a", n - 1)]
-        ev, ts_, tv = [(1, 0, consts)], 0, V_LAG
-        for w, k in turns(len(S_CH)):
-            if w == "g":
-                ev.append((ts_, 0, lambda k=k: s_gather(k)))
-                ts_ += 60 + 200 * S_CH[k]
-                ev.append((ts_, 1, lambda k=k: s_sub(k)))
-                if k < 2:
-                    ev.append((2 + k, 1, lambda k=k: s_pre(k)))
+        def first(who, p0, n, sb):
+            lo, hi = 128 * p0, 128 * (p0 + n)
+            if who == "V":
+                turn(who, tt(a("dd", lo, hi), ind(X, a("co", 8 * p0, 8 * (p0 + n))), a("yy", 0, hi - lo), OP.subtract))
+                keys("dd", p0, n, 16)
             else:
-                ev.append((ts_, 2, lambda k=k: s_abs(k)))
-                ts_ += 60 + 128 * S_CH[k]
-                if k + 2 < len(S_CH):
-                    ev.append((ts_, 0, lambda k=k: s_pre(k + 2)))
-                ev.append((ts_ + 1, 3, lambda k=k: keys("rl", sm[k], sm[k + 1], 8)))
-        for w, k in turns(len(V_CH)):
-            if w == "g":
-                ev.append((tv, 0, lambda k=k: v_gather(k)))
-                tv += 50 + 200 * V_CH[k]
-                ev.append((tv + (LATE if k < len(V_CH) - 2 else 0), 3, lambda k=k: keys("dd", vm[k], vm[k + 1], 24)))
+                turn(who, act(a("dd", lo, hi), ind(X, a("co", 8 * p0, 8 * (p0 + n)))))
+                for k in range(0, hi - lo, YW):
+                    e = min(k + YW, hi - lo)
+                    mm(A(sb, k, e), A("nid"), a("yy", 0, e - k), True, False)
+                    mm(A(sb, k, e), IDN, a("dd", lo + k, lo + e), False, True)
+
+        def second(who, p0, n, sb):
+            lo, hi = 128 * p0, 128 * (p0 + n)
+            if who == "V":
+                turn(who, ts(a("rl", lo, hi), a("dd", lo, hi), 0.0, OP.max))
+                keys("rl", p0, n, 8)
             else:
-                ev.append((tv, 2, lambda k=k: v_relu(k)))
-                tv += 64 * V_CH[k]
-                ev.append((tv + (LATE if k < len(V_CH) - 2 else END if k == len(V_CH) - 1 else 0), 3,
-                           lambda k=k: keys("rl", vm[k], vm[k + 1], 16)))
-        for e_ in sorted(ev, key=lambda x: x[:2]):
-            e_[2]()
-        scan(A("sk"), A("rk"), PK, OP.add, OP.min)
+                turn(who, act(a("rl", lo, hi), A(sb, 0, hi - lo), AF.Abs))
+                keys("rl", p0, n, 0)
+
+        p0, due = 0, {}
+        for who, n in CHUNKS[(H + t) % 2]:
+            sbank[0] += who == "S"
+            job = (who, p0, n, "ps%d" % (sbank[0] % 2))
+            first(*job)
+            if who in due:
+                second(*due[who])
+            due[who] = job
+            p0 += n
+        for job in due.values():
+            second(*job)
+
+    def post(H, t):
+        a = half(H)
+        st["cls"] = 1
+        last = t == RO - 1
+        X, w1, h1, bank = a("X", 0, W), 128 * (t + 1), 4 * (RO - t - 1), "ps%d" % (2 + H)
+        low = slice(0, 64)
+        scan(a("sk", part=low), A("rk", part=low), A(bank, 0, 256, part=low), OP.add, OP.min)
+        ts(a("kj"), a("sk", 31, 256, 32), 127, OP.bitwise_and)
+        tt(a("ex"), ind(a("kj"), A("cexp")), A("dm"), OP.mult)
+        mm(A(bank, 256, 260), a("ex"), A("b8", 24, 28), True, True)
+        copy(a("eo", 0, 4), A(bank, 256, 260))
+        mm(lanes("ps5", 0, 4), IDN, A("nb"), True, False)
+        mm(lanes("ps6", 0, 4), IDN, A("half"), True, False)
+        for c in range(2):
+            mm(lanes("ps6", 2 * c, 2 * c + 2), A("qs", 128 * c, 128 * c + 128), a("yy", 0, 64), False, False)
+        me, e = a("me"), a("se", 15, 64, 16)
+        tt(me, ind(a("cf"), a("eo", 0, 4)), A("dm", 0, 64), OP.mult)
+        for c in range(2):
+            mm(copy_c("ps4", c), A("qc", 128 * c, 128 * c + 128), me, True, True)
+        scan(a("se"), A("rst", 0, 64), me, OP.mult, OP.add)
+        ts(a("h16", h1, h1 + 4), e, OFF, OP.add)
+        for c in range(2):
+            mm(copy_c("ps5", c), A("qc", 128 * c, 128 * c + 128), me, False, False)
+        act(a("win", w1, w1 + 4), e)
         if not last:
-            act(col("aq", 0), PCNT, bias=R64)
-            act(col("ar", 0), col("aq", 0), bias=R64, scale=-1.0)
-            act(col("ac", 0), PCNT, bias=col("ar", 0))
-        ts(A("kj"), A("sk", 31, 256, 32), 255, OP.bitwise_and)
-        tt(A("ex"), ind(A("kj"), A("cexp")), A("dm", 0, 128), OP.mult)
-        mm(PW, A("ex"), A("b8", 0, 8), True, True)
-        mm(PN, A("idn"), A("half"), True, False)
-        mm(PN, A("idn"), A("yy", 0, 128), False, False)
-        copy(A("eo"), PW)
-        tt(A("me"), ind(A("cm"), A("eo")), A("dm", 0, 128), OP.mult)
-        mm(PE_, A("bf"), A("me"), True, True)
-        mm(PC, A("bf"), A("me"), False, False)
-        scan(A("se"), A("rst", 0, 128), A("me"), OP.mult, OP.max)
-        copy(A("h16", h0 - 8, h0), diag("se", 128))
-        if not last:
-            act(A("win", w0 + 256, w0 + 264), diag("se", 128))
-            send(2, t + 1, A("win", w0 + 256 + 128, w0 + 256 + 136), A("win", w0 + 256, w0 + 264))
-        act(A("xe"), ind(XW, A("h16", h0 - 8, h0)))
-        for ii in range(8):
-            n = 128 - 16 * ii
-            ts(("cmp", (ALL, ii, slice(0, n))), A("ps4", 16 * ii, 128), col("se", 16 * ii + 15), OP.is_equal, 8192.0, OP.mult)
-            if ii < 7:
-                mm(A("ps1", 16 * ii + 16, 128), A("bb"), ("cmp", (ALL, ii, slice(16, n))), False, False)
-            if ii == 2:
-                mm(PN, A("idn"), A("xe"), False, True)
-        mm(PC, A("tri"), ("cmp", (ALL, ALL, slice(0, 16))), False, True)
-        act(A("uu"), PN, bias=R1, scale=0.5)
-        act(A("nv"), A("uu"), bias=-R1)
-        scan(A("sc"), A("d0"), PC, OP.max, OP.min)
-        copy(A("so"), diag("sc", 128))
-        act(A("er", 128 * t, 128 * t + 128), PE_)
-        copy(ind(A("X"), A("so")), A("nv"))
+            send(H, t + 1)
+        act(a("xe"), ind(X, a("h16", h1, h1 + 4)))
+        for c in range(2):
+            mm(lanes("ps6", 2 * c, 2 * c + 2), A("qs", 128 * c, 128 * c + 128), a("xe"), False, c == 1)
+        for ib in range(4):
+            ts(("cmp", (ALL, 4 * H + ib, slice(0, 128 - 32 * ib))), lanes("ps4", ib, 4), a("se", 16 * ib + 15, 16 * ib + 16),
+               OP.is_equal, 8192.0, OP.mult)
+            if ib < 3:
+                mm(lanes("ps5", ib + 1, 4), A("qq"), ("cmp", (ALL, 4 * H + ib, slice(32, 128 - 32 * ib))), False, False)
+        for c in range(2):
+            mm(copy_c("ps5", c), A("tri", 128 * c, 128 * c + 128), ("cmp", (ALL, slice(4 * H, 4 * H + 4), slice(c, 32, 2))), False, c == 1)
+        if NV_ON_S:
+            act(a("uu"), lanes("ps6", 0, 4), bias=R1, scale=0.5)
+            act(a("nv"), a("uu"), bias=-R1)
+        else:
+            ts(a("ni"), lanes("ps6", 0, 4), 0.5, OP.mult)
+        for c in range(2):
+            scan(a("sc", 64 * c, 64 * c + 64), A("d0", 64 * c, 64 * c + 64), copy_c("ps5", c), OP.max, OP.min)
+        ts(a("so"), a("sc", 15, 128, 16), OFF, OP.add)
+        copy(ind(a("X"), a("so")), a("nv" if NV_ON_S else "ni"))
         if last:
-            dma("Y", T.yx[:], XW)
-        dma("Y", T.yr[RO - 1 - t:128:16, :], ("er", (slice(0, 128, 16), slice(128 * t, 128 * t + 128))), after=[old])
+            for q in range(4):
+                p0, r0 = 32 * q + 16 * (q % 2), 16 * (4 * H + q)
+                dma("Y", T.yx[r0:r0 + 16, :], a("X", 0, W, part=slice(p0, p0 + 16)), sem="out")
+            mm(A(bank, 256, 384, part=slice(0, 64)), a("win", w1, w1 + 64), A("idf"), True, True)
+            act(a("ry", part=slice(0, 64)), A(bank, 256, 384, part=slice(0, 64)), bias=OFF)
+            for q in range(4):
+                r0 = 16 * (4 * H + q)
+                dma("S", T.yr[r0:r0 + 16, :], a("ry", 32 * q, 32 * q + 32, part=slice(0, 64)), sem="out")
 
-    emit(g, T, ops, sent[0])
+    pre(0, 0)
+    score(0, 0)
+    pre(1, 0)
+    for t in range(RO):
+        post(0, t)
+        score(1, t)
+        if t < RO - 1:
+            pre(0, t + 1)
+        post(1, t)
+        if t < RO - 1:
+            score(0, t + 1)
+            pre(1, t + 1)
+
+    if not PLAN:
+        PLAN["deps"], PLAN["order"] = arrange(ops)
+    emit(g, T, ops, PLAN["deps"], PLAN["order"], sent[0])
 
 
-def emit(g, T, ops, sent):
-    Q = {"V": g.vector, "S": g.scalar, "P": g.tensor, "G": g, "Y": g.sync}
-    seen, know, seq, ndma = {}, {k: {} for k in Q}, {k: 0 for k in Q}, 0
+def touched(a):
+    key = (a[0], repr(a[1][1:]))
+    if key not in COLS:
+        m = np.zeros(SCRATCH[a[0]][1][1:], bool)
+        m[a[1][1:]] = True
+        COLS[key] = int.from_bytes(np.packbits(m.reshape(-1)).tobytes(), "big")
+    return COLS[key]
+
+
+def arrange(ops):
+    seen, deps, dur, lat = {}, [], [], []
     for n, o in enumerate(ops):
-        e = o["eng"]
-        deps = set(o["after"])
-        for kind in ("rd", "wr"):
-            for name, m in o[kind]:
+        rd = [(x[0], touched(x)) for x in o["ins"]] + [(x[2][0], touched(x[2])) for x in o["ins"] + o["outs"] if len(x) == 3]
+        wr = [(x[0], touched(x)) for x in o["outs"]]
+        d = set(o["after"])
+        for w, lst in ((False, rd), (True, wr)):
+            for name, m in lst:
                 for (k, km, kw) in seen.get(name, []):
-                    other = ops[k]["eng"] != e or ops[k]["dma"] or o["dma"]
-                    if name.startswith("ps") and other:
-                        deps.add(k)
-                    elif (kw or kind == "wr") and (m & km).any() and not (e == "P" and not other):
-                        deps.add(k)
+                    if name.startswith("ps"):
+                        if ops[k]["eng"] != o["eng"] or (o["eng"] == "P" and (o["acc"] is None or o["acc"] != ops[k]["acc"])):
+                            d.add(k)
+                    elif (kw or w) and not (o["dma"] and o["sem"] and o["sem"] == ops[k]["sem"]) and m & km:
+                        d.add(k)
+        for w, lst in ((False, rd), (True, wr)):
+            for name, m in lst:
+                seen.setdefault(name, []).append((n, m, w))
+        deps.append(d)
+        size = lambda x: 16 * touched(x[2]).bit_count() if len(x) == 3 else touched(x).bit_count()
+        two = all(SCRATCH[x[0]][2] in (B16, F16, U16) for x in o["outs"] + o["ins"] if size(x) > 1)
+        k, extra = o["kind"], 0.0
+        if k == "d":
+            x = (o["outs"] + o["ins"])[0]
+            t_, extra = 60.0, 1800.0 + {"ldx0": LOAD, "ldx1": 2 * LOAD}.get(o["sem"], 0.0)
+        elif k == "r":
+            t_, extra = 300.0, 2000.0
+        elif k == "m":
+            t_ = PCY * max(min(64, size(o["ins"][0])), size(o["ins"][1])) * (4 if SCRATCH[o["ins"][0][0]][2] == F else 1)
+        elif k == "g":
+            t_ = 150 + 2 * CY * size(o["outs"][0])
+        elif len(o["outs"][0]) == 3:
+            t_ = 55 + SC * size(o["outs"][0])
+        elif o["ins"] and len(o["ins"][0]) == 3:
+            t_ = 60 + GA * size(o["outs"][0])
+        else:
+            both = k == "tt" and not any(x[0].startswith("ps") for x in o["ins"])
+            t_ = CY * max(64, size(o["outs"][0]) * (2 if both else 0.5 if two and k == "c" else 1)) + (30 if k == "a" else 0)
+        dur.append(t_)
+        lat.append(extra)
+    hard = deps
+    deps = [d | set(o["soft"]) for d, o in zip(hard, ops)]
+    wait = lambda k, n: 0.0 if ops[k]["eng"] == ops[n]["eng"] == "P" or k not in hard[n] else lat[k] + WAKE
+    users = [[] for _ in ops]
+    for n, d in enumerate(deps):
+        for k in d:
+            users[k].append(n)
+    rest = [0.0] * len(ops)
+    for n in range(len(ops) - 1, -1, -1):
+        rest[n] = dur[n] + max([wait(n, u) + rest[u] for u in users[n]] + [lat[n]])
+    left = [len(d) for d in deps]
+    ready = [0.0] * len(ops)
+    avail = {e: [n for n, o in enumerate(ops) if o["eng"] == e and not deps[n]] for e in "VSPGY"}
+    free = {e: 0.0 for e in avail}
+    order = []
+    while len(order) < len(ops):
+        e = min((e for e in avail if avail[e]), key=lambda e: max(free[e], min(ready[n] for n in avail[e])))
+        t0 = max(free[e], min(ready[n] for n in avail[e]))
+        rankof = lambda n: (ops[n]["dma"] is True, ops[n]["cls"] * CLS + (-n if ops[n]["dma"] is True else rest[n]))
+        n = max((n for n in avail[e] if ready[n] <= t0 + HOLD), key=rankof)
+        if ready[n] > t0:
+            fit = [k for k in avail[e] if ready[k] <= t0 and t0 + dur[k] <= ready[n] + TOL]
+            if fit:
+                n = max(fit, key=rankof)
+        avail[e].remove(n)
+        free[e] = max(t0, ready[n]) + dur[n]
+        order.append(n)
+        for u in users[n]:
+            ready[u] = max(ready[u], free[e] + wait(n, u))
+            left[u] -= 1
+            if not left[u]:
+                avail[ops[u]["eng"]].append(u)
+    return hard, order
+
+
+def emit(g, T, ops, deps, order, sent):
+    Q = {"V": g.vector, "S": g.scalar, "P": g.tensor, "G": g, "Y": g.sync}
+    know, seq, total, ndma, lastacc = {k: {} for k in Q}, {k: 0 for k in Q}, {}, 0, {}
+    for n in order:
+        o = ops[n]
+        if o["acc"]:
+            lastacc[o["acc"]] = n
+        if o["dma"] is True:
+            if not o["sem"]:
+                o["sem"] = "dq%d" % ndma
+                ndma += 1
+            total[o["sem"]] = total.get(o["sem"], 0) + 16
+    for n in lastacc.values():
+        ops[n]["stop"] = True
+    for n in order:
+        o = ops[n]
+        e = o["eng"]
         need = {}
-        for k in deps:
-            if ops[k]["dma"] == "remote":
+        for k in deps[n]:
+            if ops[k]["dma"] == "remote" or (e == "P" and ops[k]["eng"] == "P"):
                 continue
             key, val = ops[k]["id"]
             if know[e].get(key, 0) < val and need.get(key, (0, 0))[0] < val:
@@ -429,35 +566,33 @@ def emit(g, T, ops, sent):
         if o["dma"] == "remote":
             o["id"] = None
         elif o["dma"]:
-            o["id"] = ("dq%d" % ndma, 1)
-            ndma += 1
+            o["id"] = (o["sem"], 1)
         else:
             seq[e] += 1
             o["id"] = ("c" + e, seq[e])
         o["done"] = dict(know[e])
         if o["id"]:
             o["done"][o["id"][0]] = o["id"][1]
-        for kind in ("rd", "wr"):
-            for name, m in o[kind]:
-                seen.setdefault(name, []).append((n, m, kind == "wr"))
-    count = {k: 0 for k in Q}
-    for o in ops:
+    count, waited = {k: 0 for k in Q}, set()
+    for n in order:
+        o = ops[n]
         q = Q[o["eng"]]
         for k in o["need"]:
             q.wait_ge(T.sem[ops[k]["id"][0]], ops[k]["val"])
+            waited.add(ops[k]["id"][0])
         for name, val in o["waits"]:
             q.wait_ge(T.sem[name], val)
-        r = o["call"]()
+        r = o["call"](o)
         if o["dma"] == "remote":
             continue
         if o["dma"]:
-            o["val"] = 16
-            r.then_inc(T.sem[o["id"][0]], 16)
+            o["val"] = total[o["sem"]]
+            r.then_inc(T.sem[o["sem"]], 16)
         elif o.get("signal"):
             count[o["eng"]] += 1
             o["val"] = count[o["eng"]]
             r.then_inc(T.sem[o["id"][0]], 1)
     g.wait_ge(T.sem.sent, sent)
-    for o in ops:
-        if o["dma"] is True and not o.get("signal"):
-            g.wait_ge(T.sem[o["id"][0]], 16)
+    for name, val in total.items():
+        if name not in waited:
+            g.wait_ge(T.sem[name], val)

@@ -9,12 +9,14 @@ R32 = float((1 << 28) + (1 << 23))
 R64 = float(3 << 28)
 R128 = float(3 << 29)
 OFF = 2048.0
-CHUNKS = [[(_c[0], int(_c[1])) for _c in "S2 V1 S3 V1 V1 S3 V1 V1 S1 V1 V1".split()]] * 2
-NV_ON_S = False
-EX_ON_S = False
+CHUNKS = [[(_c[0], int(_c[1])) for _c in _s.split()]
+          for _s in ("S2 V1 S3 V1 V1 S2 V1 V1 S1 V1 V1 V1", "S4 V1 S4 V1 V1 V1 V1 S1 V1 V1", "S3 V1 V1 S3 V1 V1 V1 S1 V1 V1 V1 V1")]
+NV_ON_S = True
+WIDE = False
 CY, PCY, GA, SC, WAKE, HOLD = 0.9, 0.45, 1.25, 2.7, 215.0, 230.0
-YW = 128
-CLS, TOL, LOAD = 1000.0, 100.0, 4000.0
+YW, YS = 128, 2
+GO, XAB, CF_ON_S, ONEG, WIN_ON_G, XE_ON_V, EX2 = 0, 2, False, True, True, False, True
+LOAD, PASSES, LAG, CLS, TOL, MIX = 2700.0, 4, 3800.0, 300.0, 70.0, 0.5
 F, B16, F16, I32, U16 = "float32", "bfloat16", "float16", "int32", "uint16"
 
 
@@ -27,32 +29,32 @@ HALVES = {
     "sel": (128, B16), "bsel": (128, B16),
     "xab": (128, B16), "sa": (64, F), "ao": (8, U16), "cn": (8, B16),
     "mpq": (128, F16), "spq": (256, F16), "opq": (8, U16), "pq": (8, F), "gg": (8, F), "tr": (32, F16),
-    "ci": (128, I32), "cm": (128, I32), "cf": (128, F), "co": (128, U16), "xpq": (128, B16), "yy": (256, B16),
+    "ci": (128, I32), "cm": (128, I32), "cf": (128, F), "co": (128, U16), "xpq": (128, B16), "yy": (512, B16),
     "dd": (W // 2, B16), "rl": (W // 2, B16), "sk": (256, I32), "ex": (128, B16), "kj": (8, I32),
     "eo": (8, U16), "me": (64, F16), "se": (64, F), "sc": (128, F), "so": (8, U16), "xe": (64, B16),
-    "uu": (128, F), "nv": (128, B16), "ni": (128, I32), "ry": (128, F),
+    "exf": (128, F), "nv": (128, B16), "ni": (128, I32), "ry": (128, F),
 }
 SCRATCH = {_n: _sb(2 * _v[0], _v[1]) for _n, _v in HALVES.items()}
 SCRATCH.update({
-    "cmp": _sb([8, 128], B16), "R": _sb([2, 4, 32], F16), "mc": _sb(192, B16),
+    "cmp": _sb([8, 128], B16), "R": _sb([2, 4, 32], F16), "mc": _sb(320, B16),
     "rin": _sb(128, I32), "r16": _sb(128, F16), "wti": _sb(4, I32), "kpi": _sb(4, I32), "kpj": _sb(4, I32),
-    "pc": _sb(8, I32), "pf": _sb(16, F), "j8": _sb(8, F), "jp": _sb(128, B16), "jg": _sb(128, B16),
+    "pc": _sb(12, I32), "pf": _sb(20, F), "cex4": _sb(8, U16), "mx": _sb(32, B16), "lc": _sb(64, B16), "bf": _sb(8, F), "j8": _sb(8, F), "jp": _sb(128, B16), "jg": _sb(128, B16),
     "jq": _sb(128, B16), "jc": _sb(128, B16), "j16": _sb(128, B16), "i8": _sb(64, F), "j4": _sb(64, F),
     "i4m": _sb(256, B16), "odd": _sb(64, F), "w4": _sb(8, B16), "wf": _sb(4, F), "kf": _sb(8, F), "km": _sb(64, F16),
-    "pk": _sb(8, F), "sl": _sb(8, F), "cs": _sb(8, F), "c1": _sb(64, F), "c2": _sb(64, F), "g0": _sb(128, B16),
+    "pk": _sb(8, F), "sl": _sb(8, F), "cs": _sb(8, F), "ch": _sb(8, F), "c1": _sb(64, F), "c2": _sb(64, F), "g0": _sb(128, B16),
     "g1": _sb(128, B16), "g2": _sb(128, B16),
     "idn": _sb([2, 4, 16], B16), "nid": _sb(128, B16), "idf": _sb(128, F), "dm": _sb(128, B16),
     "nb": _sb(128, B16), "bb": _sb(128, B16), "qq": _sb(128, B16), "qc": _sb(256, B16), "qs": _sb(256, B16),
     "tri": _sb(256, B16), "b8": _sb(32, B16), "ca": _sb(128, B16), "rs8": _sb(64, F),
-    "rst": _sb(128, B16), "rk": _sb(256, F), "d0": _sb(128, F), "ck": _sb(256, B16), "cexp": _sb(8, U16),
+    "rst": _sb(128, B16), "rk": _sb(256, F), "d0": _sb(128, F), "ck": _sb(256, B16), "cexp": _sb(8, U16), "same": _sb(8, U16), "cex2": _sb(8, U16), "b8f": _sb(8, F),
     "one": _sb(128, B16), "half": _sb(128, B16),
     "junk": _sb(16, F), "cnt": _sb(4, F), "aq": _sb(4, F), "ar": _sb(4, F), "ac": _sb(4, F),
 })
 for _k in range(8):
     SCRATCH["ps%d" % _k] = ("psum", [128, 512], F)
 
-SEMAPHORES = (["cV", "cS", "cP", "cG", "sent"] + ["arr%d" % _t for _t in range(2 * RO)]
-              + ["ldx0", "ldx1", "out"] + ["dq%d" % _k for _k in range(16)])
+SEMAPHORES = (["cV", "cS", "cP", "cG", "sent", "go"] + ["arr%d" % _t for _t in range(2 * RO)]
+              + ["ldx0", "ldx1", "out0", "out1"] + ["dq%d" % _k for _k in range(16)])
 COLS = {}
 PLAN = {}
 
@@ -87,6 +89,9 @@ def rank_program(g, core, T, topo):
         o = {"eng": eng, "kind": kind, "call": call, "outs": outs, "ins": [a for a in ins if isinstance(a, tuple)],
              "dma": False, "after": [], "soft": [], "waits": [], "acc": None, "stop": False, "cls": st["cls"], "sem": None}
         o.update(kw)
+        key = (st.get("part"), eng)
+        st[key] = st.get(key, 0) + 1
+        o["tag"] = st["part"] + (eng, st[key]) if st.get("part") else None
         ops.append(o)
         return len(ops) - 1
 
@@ -133,13 +138,19 @@ def rank_program(g, core, T, topo):
         a = half(H)
         peer = T.cores[(rank - 1 - t) % N]
         rid, pid, _se = topo.addr(peer)
-        sent[0] += len(topo.engines(core, peer))
+        es = topo.engines(core, peer)[H::2]
+        sent[0] += len(es)
         src, dst = a("win", 128 * t, 128 * t + 64), a("win", 128 * t + 64, 128 * t + 128)
-        sends[H, t] = add("G", "r", lambda _o: g.remote_dma(ap(dst), ap(src), T.sem["arr%d" % (2 * t + H)], T.sem.sent, pid, rid,
-                                                            topo.mask(core, peer)), [], [src], dma="remote")
+
+        def call(_o):
+            g.remote_dma(ap(dst), ap(src), T.sem["arr%d" % (2 * t + H)], T.sem.sent, pid, rid, sum(1 << e for e in es))
+            if (H, t) == (GO, 0):
+                g.sem_inc(T.sem.go, 1)
+
+        sends[H, t] = add("G", "r", call, [], [src], dma="remote", first=(H, t) == (0, 0))
 
     def arrival(H, t):
-        return ("arr%d" % (2 * t + H), len(topo.engines(T.cores[(rank + 1 + t) % N], core)))
+        return ("arr%d" % (2 * t + H), len(topo.engines(T.cores[(rank + 1 + t) % N], core)[H::2]))
 
     col = lambda name, j: A(name, j, j + 1)
     IDN = ("idn", (ALL, ALL, ALL, ALL))
@@ -148,16 +159,19 @@ def rank_program(g, core, T, topo):
     copy_c = lambda bank, c: A(bank, c, 128, 2)
 
     def load_x(H):
-        for q in range(4):
-            for c in range(2):
-                p0, r0 = 32 * q + 16 * c, 16 * (4 * H + q)
-                dma("YS"[c], half(H)("X", 0, W, part=slice(p0, p0 + 16)), T.x[r0:r0 + 16, :], sem="ldx%d" % H)
+        for k, (p0, p1) in enumerate(((16, 48), (48, 80), (80, 112), (0, 16), (112, 128))):
+            r0 = 64 * H + 16 * (p0 // 32)
+            n = dma("YS"[k % 2 * (1 - H)], half(H)("X", 0, W, part=slice(p0, p1)), T.x[r0:r0 + p1 - p0, :], sem="ldx%d" % H)
+            if H == 1:
+                ops[n]["soft"].append(sends[GO, 0])
+                ops[n]["waits"] = [("go", 1)] if k == 0 else []
+                if k:
+                    ops[n]["soft"].append(n - 1)
 
     dma("Y", A("rin"), T.ring[:])
     dma("S", A("wti", 0, 1), T.wt[:])
     load_x(0)
     dma("S", A("kpi", 0, 2), T.kap[:])
-    load_x(1)
 
     iota(col("pc", 0), [[0, 1]], 0, 1)
     iota(A("jp"), [[1, 128]], 0, 0)
@@ -181,7 +195,7 @@ def rank_program(g, core, T, topo):
     copy(A("pf", 1, 8), A("pc", 1, 8))
     p_, pg_, r_, q_, hi_, kind_, s7_ = [col("pf", j) for j in (0, 1, 2, 3, 5, 6, 7)]
     ts(IDN, A("jp"), p_, OP.is_equal)
-    fill(A("half"), -0.5)
+    fill(A("half"), -0.25)
     fill(A("one"), 1.0)
     ts(A("r16"), A("rin"), -OFF, OP.add)
     for q in range(4):
@@ -191,6 +205,7 @@ def rank_program(g, core, T, topo):
         act(half(H)("win", 0, 64), A("ps7", 64 * H, 64 * H + 64))
         send(H, 0)
         ts(half(H)("h16", 4 * RO, 4 * RO + 8), half(H)("win", 0, 8), OFF, OP.add)
+    load_x(1)
     ts(col("pf", 8), p_, -64.0, OP.add)
     ts(col("pf", 9), pg_, -4.0, OP.add)
     ts(col("w4", 0), col("wti", 0), 4.0, OP.mult)
@@ -212,6 +227,7 @@ def rank_program(g, core, T, topo):
     ts(A("rs8"), A("i8"), 1.0, OP.min)
     for k, c in enumerate((R128, 2 * R128, 127.5)):
         act(A("mc", 64 * k, 64 * k + 64), A("one", 0, 64), scale=c)
+    act(A("mc", 192, 320), A("one"), scale=R1)
     act(A("rst"), A("one"))
     act(A("rst", 0, 128, 16), A("one", 0, 8), scale=0.0)
     ts(A("kpj", 0, 2), A("kpi", 0, 2), 1, OP.bitwise_and)
@@ -227,6 +243,7 @@ def rank_program(g, core, T, topo):
     ts(A("pk"), A("j8"), kind_, OP.is_equal)
     ts(A("sl"), A("j8"), s7_, OP.is_equal)
     ts(A("cs"), A("j8"), col("pf", 4), OP.is_equal)
+    ts(A("ch"), A("j8"), col("pf", 4), OP.is_equal, 0.5, OP.mult)
     act(A("odd"), A("odd"), scale=col("pk", 1))
     act(A("c1"), lanes("ps5", 0, 2), scale=col("pk", 0))
     act(A("c2"), lanes("ps5", 2, 4), scale=col("pk", 2))
@@ -244,6 +261,7 @@ def rank_program(g, core, T, topo):
         act(copy_c("nb", c), A("dm", 0, 64), bias=BIG, scale=-BIG)
     for k, s in enumerate((128.0, 256.0, -128.0, 1.0)):
         act(A("b8", 8 * k, 8 * k + 8), A("bb", 0, 128, 16), scale=s)
+    act(A("bf"), A("bb", 0, 128, 16))
     ts(A("ck"), A("i4m"), pg_, OP.add)
     fill(A("rk"), 0.0)
     act(A("rk", 0, 256, 32), A("one", 0, 8), scale=BIG)
@@ -251,6 +269,20 @@ def rank_program(g, core, T, topo):
     ts(col("pf", 10), r_, W - OFF, OP.add)
     ts(A("d0", 0, 128, 16), A("j8"), 16.0, OP.mult, col("pf", 10), OP.add)
     copy(A("cexp"), A("j8"))
+    if EX2:
+        ts(col("pc", 8), col("pc", 0), 2, OP.arith_shift_right, 3, OP.bitwise_and)
+        copy(col("pf", 16), col("pc", 8))
+        ts(A("cex4", 0, 2), A("j8", 0, 2), 4.0, OP.mult, col("pf", 16), OP.add)
+        for k in range(4):
+            act(A("mx", k, 32, 4), A("one", 0, 8), scale=col("bf", k))
+        act(A("lc"), A("one", 0, 64), scale=0.0)
+        for k in (0, 48):
+            act(A("lc", k, k + 16), A("dm", 0, 16))
+    ts(A("same"), A("j8"), 16.0, OP.mult, r_, OP.add)
+    if WIDE:
+        ts(A("cex2"), A("j8"), 16.0, OP.mult, 15.0, OP.add)
+        for m2 in range(2):
+            act(A("b8f", m2, 8, 2), A("bb", 64 * m2, 64 * m2 + 64, 16))
     ts(A("qq"), A("jq"), q_, OP.is_equal)
     ts(col("pf", 11), q_, 16.0, OP.mult, r_, OP.add)
     ts(col("pf", 12), q_, 16.0, OP.mult, 15.0, OP.add)
@@ -260,7 +292,7 @@ def rank_program(g, core, T, topo):
     tt(col("pf", 14), col("pf", 14), col("pf", 15), OP.add)
     for c in range(2):
         act(A("qc", 128 * c, 128 * c + 128), A("qq"), scale=col("cs", c))
-        ts(A("qs", 128 * c, 128 * c + 128), A("jc"), col("pf", 11), OP.is_equal, col("cs", c), OP.mult)
+        ts(A("qs", 128 * c, 128 * c + 128), A("jc"), col("pf", 11), OP.is_equal, col("ch", c), OP.mult)
     ts(A("g0"), A("jc"), col("pf", 13), OP.is_gt)
     ts(A("g1"), A("jc"), col("pf", 14), OP.is_gt)
     tt(A("tri", 0, 128), A("g0"), A("qq"), OP.mult)
@@ -270,12 +302,18 @@ def rank_program(g, core, T, topo):
 
     def pre(H, t):
         a = half(H)
-        st["cls"] = 1
+        st["cls"], st["part"] = 1, (H, t, "pre")
         X, w0, h0 = a("X", 0, W), 128 * t, 4 * (RO - t)
         own = "ps%d" % (2 + H)
-        PA, PY, PS = A(own, 0, 64), A("ps6", 0, 64), lambda *s, **k: A("ps7", *s, **k)
+        PA, PY, PS = A(own, 0, 64), A("ps4", 0, 64), lambda *s, **k: A("ps7", *s, **k)
         dma("Y", a("win", w0 + 132, w0 + 192), a("win", w0, w0 + 60), sem="dq%d" % (3 + 2 * t + H))
-        act(a("xab"), ind(X, a("h16", h0, h0 + 8)))
+        if XAB == 2:
+            copy(a("xab", 0, 64), ind(X, a("h16", h0, h0 + 4)))
+            act(a("xab", 64, 128), ind(X, a("h16", h0 + 4, h0 + 8)))
+        elif XAB == 1:
+            copy(a("xab"), ind(X, a("h16", h0, h0 + 8)))
+        else:
+            act(a("xab"), ind(X, a("h16", h0, h0 + 8)))
         mm(PA, IDN, A("ca", 0, 64), True, False)
         for k in (2, 3):
             mm(PA, a("wb", 128 * k, 128 * k + 128), a("xab", k % 2, 128, 2), False, False)
@@ -293,7 +331,9 @@ def rank_program(g, core, T, topo):
         ts(a("opq"), a("spq", 15, 128, 16), OFF, OP.add)
         for k, bank in enumerate(("ps7", own)):
             for q in range(4):
-                mm(A(bank, 0, 64, part=quad(q)), a("tr", part=quad(q)), ("R", (quad(q), H, slice(2 * k, 2 * k + 2), ALL)), True, True)
+                n = mm(A(bank, 0, 64, part=quad(q)), a("tr", part=quad(q)), ("R", (quad(q), H, slice(2 * k, 2 * k + 2), ALL)), True, True)
+                if k:
+                    ops[n]["soft"].append(n - 1)
         ts(a("gg", 0, 4), a("pq", 0, 4), -1007.5 if t == 0 else col("ac", t % 2), OP.add, R32, OP.add)
         act(a("xpq"), ind(X, a("opq")))
         mm(PY, IDN, A("mc", 128, 192), True, False)
@@ -309,15 +349,20 @@ def rank_program(g, core, T, topo):
             ts(a("cm", 64 * k, 64 * k + 64), a("ci", 64 * k, 64 * k + 64), 5, OP.arith_shift_right, W - 1, OP.bitwise_and)
         for k in range(2):
             copy(a("co", 64 * k, 64 * k + 64), a("cm", 64 * k, 64 * k + 64))
-        for k in range(YW // 64):
+        for k in range(YS):
             act(a("yy", 64 * k, 64 * k + 64), PY)
+        for k in range(64 * YS, YW, 128):
+            copy(a("yy", k, k + 128), a("yy", 0, 128))
         st["cls"] = 0
-        ts(a("cf"), a("cm"), -OFF, OP.add)
+        if CF_ON_S:
+            act(a("cf"), ind(a("cm"), A("same")), bias=-OFF)
+        else:
+            ts(a("cf"), a("cm"), -OFF, OP.add)
         if t < RO - 1:
-            ts(a("cn"), a("sa", 7, 64, 8), 64.0, OP.is_ge)
+            act(a("cn"), a("sa", 7, 64, 8), AF.Sign, bias=-63.5)
             mm(PS(256 + 8 * H, 264 + 8 * H), A("one"), a("cn"), True, True)
             if H == 1:
-                act(A("junk"), PS(256, 272), bias=-(31 + 15.5 / 32) / 16, acc=col("cnt", 0))
+                act(A("junk"), PS(256, 272), bias=64 - (31 + 15.5 / 32) / 16, scale=0.5, acc=col("cnt", 0))
                 act(col("aq", 0), col("cnt", 0), bias=R64)
                 act(col("ar", 0), col("aq", 0), bias=32 * R64, scale=-32.0)
                 act(col("ac", (t + 1) % 2), col("cnt", 0), bias=col("ar", 0), scale=32.0)
@@ -325,9 +370,12 @@ def rank_program(g, core, T, topo):
     def score(H, t):
         a = half(H)
         X, bank, grp = a("X", 0, W), "ps%d" % (2 + H), (H, t)
-        st["cls"] = 1
+        st["cls"], st["part"] = 1, (H, t, "score")
         low = slice(0, 64)
-        mm(A(bank, 0, 256, part=low), ("idn", (ALL, 0, ALL, ALL)), A("ck"), True, False)
+        if WIDE:
+            mm(A(bank, 0, 128), IDN, A("ck", 0, 256, 2), True, False)
+        else:
+            mm(A(bank, 0, 256, part=low), ("idn", (ALL, 0, ALL, ALL)), A("ck"), True, False)
         st["cls"] = 0
         line = {}
 
@@ -337,24 +385,36 @@ def rank_program(g, core, T, topo):
             line[who] = n
 
         def keys(buf, p0, n, c):
-            for m in range(2 * p0, 2 * (p0 + n)):
+            for mp in range(p0, p0 + n) if WIDE else ():
+                mm(A(bank, mp, 128, 16), a(buf, 128 * mp, 128 * mp + 128), A("b8", c, c + 8), False, False, acc=grp)
+            for m in () if WIDE else range(2 * p0, 2 * (p0 + n)):
                 mm(A(bank, m, 256, 32, part=low), a(buf, 64 * m, 64 * m + 64), A("b8", c, c + 8), False, False, acc=grp)
 
         def first(who, p0, n, sb):
             lo, hi = 128 * p0, 128 * (p0 + n)
-            if who == "V":
+            if who == "W":
+                for k in range(n):
+                    turn("V", tt(a("dd", lo + 128 * k, lo + 128 * k + 128), ind(X, a("co", 8 * (p0 + k), 8 * (p0 + k + 1))),
+                                 a("yy", 0, 128), OP.subtract))
+            elif who == "V":
                 turn(who, tt(a("dd", lo, hi), ind(X, a("co", 8 * p0, 8 * (p0 + n))), a("yy", 0, hi - lo), OP.subtract))
                 keys("dd", p0, n, 16)
             else:
                 turn(who, act(a("dd", lo, hi), ind(X, a("co", 8 * p0, 8 * (p0 + n)))))
                 for k in range(0, hi - lo, YW):
                     e = min(k + YW, hi - lo)
-                    mm(A(sb, k, e), A("nid"), a("yy", 0, e - k), True, False)
-                    mm(A(sb, k, e), IDN, a("dd", lo + k, lo + e), False, True)
+                    mm(A(sb, k, e), A("nid"), a("yy", 0, e - k), k == 0 or not ONEG, False)
+                    if not ONEG:
+                        mm(A(sb, k, e), IDN, a("dd", lo + k, lo + e), False, True)
+                if ONEG:
+                    mm(A(sb, 0, hi - lo), IDN, a("dd", lo, hi), False, True)
 
         def second(who, p0, n, sb):
             lo, hi = 128 * p0, 128 * (p0 + n)
-            if who == "V":
+            if who == "W":
+                act(a("rl", lo, hi), a("dd", lo, hi), AF.Abs)
+                keys("rl", p0, n, 0)
+            elif who == "V":
                 turn(who, ts(a("rl", lo, hi), a("dd", lo, hi), 0.0, OP.max))
                 keys("rl", p0, n, 8)
             else:
@@ -362,7 +422,7 @@ def rank_program(g, core, T, topo):
                 keys("rl", p0, n, 0)
 
         p0, due = 0, {}
-        for who, n in CHUNKS[(H + t) % 2]:
+        for who, n in CHUNKS[2 if (H, t) == (1, RO - 1) else H]:
             sbank[0] += who == "S"
             job = (who, p0, n, "ps%d" % (sbank[0] % 2))
             first(*job)
@@ -375,15 +435,30 @@ def rank_program(g, core, T, topo):
 
     def post(H, t):
         a = half(H)
-        st["cls"] = 1
+        st["cls"], st["part"] = 1, (H, t + 1, "post")
         last = t == RO - 1
         X, w1, h1, bank = a("X", 0, W), 128 * (t + 1), 4 * (RO - t - 1), "ps%d" % (2 + H)
         low = slice(0, 64)
-        scan(a("sk", part=low), A("rk", part=low), A(bank, 0, 256, part=low), OP.add, OP.min)
-        ts(a("kj"), a("sk", 31, 256, 32), 127, OP.bitwise_and)
-        tt(a("ex"), ind(a("kj"), A("cexp")), A("dm"), OP.mult)
-        mm(A(bank, 256, 260), a("ex"), A("b8", 24, 28), True, True)
-        copy(a("eo", 0, 4), A(bank, 256, 260))
+        if WIDE:
+            scan(a("sk", 0, 128), A("rk", 0, 256, 2), A(bank, 0, 128), OP.add, OP.min)
+            tt(a("exf"), ind(a("sk", 0, 128), A("cex2")), A("dm"), OP.mult)
+            mm(A(bank, 128, 136), a("exf"), A("b8f"), True, True)
+            scan(a("sk", 128, 136), A("rk", 0, 128, 16), A(bank, 128, 136), OP.add, OP.min)
+            ts(a("kj", 0, 4), a("sk", 129, 136, 2), 127, OP.bitwise_and)
+            copy(a("eo", 0, 4), a("kj", 0, 4))
+        else:
+            scan(a("sk", part=low), A("rk", part=low), A(bank, 0, 256, part=low), OP.add, OP.min)
+            ts(a("kj"), a("sk", 31, 256, 32), 127, OP.bitwise_and)
+            if EX2:
+                tt(a("ex", 0, 32), ind(a("kj"), A("cex4", 0, 2)), A("mx"), OP.mult)
+                for q in range(4):
+                    for c in range(2):
+                        j = 8 * q + 4 * c
+                        mm(A(bank, 256, 260, part=quad(q)), A("lc", 32 * c, 32 * c + 32, part=low), a("ex", j, j + 4, part=low), c == 0, c == 1)
+            else:
+                tt(a("ex"), ind(a("kj"), A("cexp")), A("dm"), OP.mult)
+                mm(A(bank, 256, 260), a("ex"), A("b8", 24, 28), True, True)
+            copy(a("eo", 0, 4), A(bank, 256, 260))
         mm(lanes("ps5", 0, 4), IDN, A("nb"), True, False)
         mm(lanes("ps6", 0, 4), IDN, A("half"), True, False)
         for c in range(2):
@@ -391,42 +466,48 @@ def rank_program(g, core, T, topo):
         me, e = a("me"), a("se", 15, 64, 16)
         tt(me, ind(a("cf"), a("eo", 0, 4)), A("dm", 0, 64), OP.mult)
         for c in range(2):
-            mm(copy_c("ps4", c), A("qc", 128 * c, 128 * c + 128), me, True, True)
+            mm(copy_c(bank, c), A("qc", 128 * c, 128 * c + 128), me, True, True)
         scan(a("se"), A("rst", 0, 64), me, OP.mult, OP.add)
         ts(a("h16", h1, h1 + 4), e, OFF, OP.add)
         for c in range(2):
             mm(copy_c("ps5", c), A("qc", 128 * c, 128 * c + 128), me, False, False)
-        act(a("win", w1, w1 + 4), e)
+        if WIN_ON_G:
+            new = a("win", w1, w1 + 4)
+            add("G", "g", lambda _o: g.affine_select(ap(new), ap(e), [[0, 4]], OP.is_ge, 0.0, 0, 0), [new], [e])
+        else:
+            act(a("win", w1, w1 + 4), e)
         if not last:
             send(H, t + 1)
-        act(a("xe"), ind(X, a("h16", h1, h1 + 4)))
+        (copy if XE_ON_V else act)(a("xe"), ind(X, a("h16", h1, h1 + 4)))
         for c in range(2):
-            mm(lanes("ps6", 2 * c, 2 * c + 2), A("qs", 128 * c, 128 * c + 128), a("xe"), False, c == 1)
+            mm(lanes("ps6", 2 * c, 2 * c + 2), A("qs", 128 * c, 128 * c + 128), a("xe"), False, c == 1 and not NV_ON_S)
+        if NV_ON_S:
+            mm(lanes("ps6", 0, 4), IDN, A("mc", 192, 320), False, False)
+            mm(lanes("ps6", 0, 4), A("nid"), A("mc", 192, 320), False, True)
         for ib in range(4):
-            ts(("cmp", (ALL, 4 * H + ib, slice(0, 128 - 32 * ib))), lanes("ps4", ib, 4), a("se", 16 * ib + 15, 16 * ib + 16),
+            ts(("cmp", (ALL, 4 * H + ib, slice(0, 128 - 32 * ib))), lanes(bank, ib, 4), a("se", 16 * ib + 15, 16 * ib + 16),
                OP.is_equal, 8192.0, OP.mult)
             if ib < 3:
                 mm(lanes("ps5", ib + 1, 4), A("qq"), ("cmp", (ALL, 4 * H + ib, slice(32, 128 - 32 * ib))), False, False)
         for c in range(2):
             mm(copy_c("ps5", c), A("tri", 128 * c, 128 * c + 128), ("cmp", (ALL, slice(4 * H, 4 * H + 4), slice(c, 32, 2))), False, c == 1)
         if NV_ON_S:
-            act(a("uu"), lanes("ps6", 0, 4), bias=R1, scale=0.5)
-            act(a("nv"), a("uu"), bias=-R1)
+            act(a("nv"), lanes("ps6", 0, 4))
         else:
-            ts(a("ni"), lanes("ps6", 0, 4), 0.5, OP.mult)
+            copy(a("ni"), lanes("ps6", 0, 4))
         for c in range(2):
             scan(a("sc", 64 * c, 64 * c + 64), A("d0", 64 * c, 64 * c + 64), copy_c("ps5", c), OP.max, OP.min)
         ts(a("so"), a("sc", 15, 128, 16), OFF, OP.add)
         copy(ind(a("X"), a("so")), a("nv" if NV_ON_S else "ni"))
         if last:
-            for q in range(4):
-                p0, r0 = 32 * q + 16 * (q % 2), 16 * (4 * H + q)
-                dma("Y", T.yx[r0:r0 + 16, :], a("X", 0, W, part=slice(p0, p0 + 16)), sem="out")
+            for k in range(2):
+                r0 = 64 * H + 32 * k
+                dma("Y", T.yx[r0:r0 + 32, :], a("X", 0, W, part=slice(64 * k + 16, 64 * k + 48)), sem="out%d" % H)
             mm(A(bank, 256, 384, part=slice(0, 64)), a("win", w1, w1 + 64), A("idf"), True, True)
             act(a("ry", part=slice(0, 64)), A(bank, 256, 384, part=slice(0, 64)), bias=OFF)
             for q in range(4):
                 r0 = 16 * (4 * H + q)
-                dma("S", T.yr[r0:r0 + 16, :], a("ry", 32 * q, 32 * q + 32, part=slice(0, 64)), sem="out")
+                dma("S", T.yr[r0:r0 + 16, :], a("ry", 32 * q, 32 * q + 32, part=slice(0, 64)), sem="out%d" % H)
 
     pre(0, 0)
     score(0, 0)
@@ -442,6 +523,9 @@ def rank_program(g, core, T, topo):
             pre(1, t + 1)
 
     if not PLAN:
+        loads = [n for n, o in enumerate(ops) if o["dma"] is True][:8]
+        for k, n in zip(loads, loads[1:]):
+            ops[n]["soft"].append(k)
         PLAN["deps"], PLAN["order"] = arrange(ops)
     emit(g, T, ops, PLAN["deps"], PLAN["order"], sent[0])
 
@@ -463,8 +547,13 @@ def arrange(ops):
         d = set(o["after"])
         for w, lst in ((False, rd), (True, wr)):
             for name, m in lst:
-                for (k, km, kw) in seen.get(name, []):
+                runs = []
+                for (k, km, kw) in reversed(seen.get(name, [])):
                     if name.startswith("ps"):
+                        if not runs or runs[-1] != (ops[k]["eng"], ops[k]["acc"]):
+                            runs.append((ops[k]["eng"], ops[k]["acc"]))
+                            if len(runs) > 2:
+                                break
                         if ops[k]["eng"] != o["eng"] or (o["eng"] == "P" and (o["acc"] is None or o["acc"] != ops[k]["acc"])):
                             d.add(k)
                     elif (kw or w) and not (o["dma"] and o["sem"] and o["sem"] == ops[k]["sem"]) and m & km:
@@ -478,9 +567,9 @@ def arrange(ops):
         k, extra = o["kind"], 0.0
         if k == "d":
             x = (o["outs"] + o["ins"])[0]
-            t_, extra = 60.0, 1800.0 + {"ldx0": LOAD, "ldx1": 2 * LOAD}.get(o["sem"], 0.0)
+            t_, extra = 60.0, 1800.0 + {"ldx0": LOAD, "ldx1": LOAD}.get(o["sem"], 0.0)
         elif k == "r":
-            t_, extra = 300.0, 2000.0
+            t_, extra = 300.0, 3500.0 if o["first"] else 2000.0
         elif k == "m":
             t_ = PCY * max(min(64, size(o["ins"][0])), size(o["ins"][1])) * (4 if SCRATCH[o["ins"][0][0]][2] == F else 1)
         elif k == "g":
@@ -502,31 +591,64 @@ def arrange(ops):
         for k in d:
             users[k].append(n)
     rest = [0.0] * len(ops)
-    for n in range(len(ops) - 1, -1, -1):
-        rest[n] = dur[n] + max([wait(n, u) + rest[u] for u in users[n]] + [lat[n]])
-    left = [len(d) for d in deps]
-    ready = [0.0] * len(ops)
-    avail = {e: [n for n, o in enumerate(ops) if o["eng"] == e and not deps[n]] for e in "VSPGY"}
-    free = {e: 0.0 for e in avail}
-    order = []
-    while len(order) < len(ops):
-        e = min((e for e in avail if avail[e]), key=lambda e: max(free[e], min(ready[n] for n in avail[e])))
-        t0 = max(free[e], min(ready[n] for n in avail[e]))
-        rankof = lambda n: (ops[n]["dma"] is True, ops[n]["cls"] * CLS + (-n if ops[n]["dma"] is True else rest[n]))
-        n = max((n for n in avail[e] if ready[n] <= t0 + HOLD), key=rankof)
-        if ready[n] > t0:
-            fit = [k for k in avail[e] if ready[k] <= t0 and t0 + dur[k] <= ready[n] + TOL]
-            if fit:
-                n = max(fit, key=rankof)
-        avail[e].remove(n)
-        free[e] = max(t0, ready[n]) + dur[n]
-        order.append(n)
-        for u in users[n]:
-            ready[u] = max(ready[u], free[e] + wait(n, u))
-            left[u] -= 1
-            if not left[u]:
-                avail[ops[u]["eng"]].append(u)
-    return hard, order
+    tail = list(lat)
+    choice = [[n for n, o in enumerate(ops) if o["tag"] == (H, RO, "post", "V", 1)][0] for H in range(2)]
+    for _ in range(2):
+        for n in range(len(ops) - 1, -1, -1):
+            rest[n] = dur[n] + max([wait(n, u) + rest[u] for u in users[n]] + [tail[n]])
+        tail[choice[0]] = rest[choice[1]] - dur[choice[1]] + LAG
+    before = [[(k, wait(k, n)) for k in d] for n, d in enumerate(deps)]
+    behind = [[(u, wait(n, u)) for u in users[n]] for n in range(len(ops))]
+
+    def place(turn, needs, lead):
+        end, busy = [0.0] * len(ops), {e: [] for e in "VSPGY"}
+        for n in turn:
+            t0 = max([end[k] + w for k, w in needs[n]] + [lead[n]])
+            b = busy[ops[n]["eng"]]
+            j = len(b)
+            while j and b[j - 1][1] > t0:
+                j -= 1
+            while j < len(b) and t0 + dur[n] > b[j][0]:
+                t0 = max(t0, b[j][1])
+                j += 1
+            b.insert(j, (t0, t0 + dur[n]))
+            end[n] = t0 + dur[n]
+        return end
+
+    def greedy(rank, needs, gives, lead):
+        left, ready, end = [len(d) for d in needs], list(lead), [0.0] * len(ops)
+        avail = {e: [n for n, o in enumerate(ops) if o["eng"] == e and not needs[n]] for e in "VSPGY"}
+        free, order = {e: 0.0 for e in avail}, []
+        while len(order) < len(ops):
+            e = min((e for e in avail if avail[e]), key=lambda e: max(free[e], min(ready[n] for n in avail[e])))
+            t0 = max(free[e], min(ready[n] for n in avail[e]))
+            n = max((n for n in avail[e] if ready[n] <= t0 + HOLD), key=lambda n: rank[n])
+            if ready[n] > t0:
+                fit = [k for k in avail[e] if ready[k] <= t0 and t0 + dur[k] <= ready[n] + TOL]
+                if fit:
+                    n = max(fit, key=lambda n: rank[n])
+            avail[e].remove(n)
+            end[n] = free[e] = max(t0, ready[n]) + dur[n]
+            order.append(n)
+            for u, w in gives[n]:
+                ready[u] = max(ready[u], free[e] + w)
+                left[u] -= 1
+                if not left[u]:
+                    avail[ops[u]["eng"]].append(u)
+        return order, end
+
+    calls, none, best = range(len(ops)), [0.0] * len(ops), None
+    rank = [rest[n] + CLS * ops[n]["cls"] for n in calls]
+    for _ in range(PASSES):
+        order, end = greedy(rank, before, behind, none)
+        span = max(end[n] + lat[n] for n in calls)
+        if best is None or span < best[0]:
+            best = (span, order)
+        back = greedy(end, behind, before, tail)[1]
+        rank = [MIX * back[n] + (1 - MIX) * rank[n] for n in calls]
+    PLAN["span"] = best[0]
+    PLAN["dbg"] = (ops, rest, behind, dur, greedy, before, tail)
+    return hard, best[1]
 
 
 def emit(g, T, ops, deps, order, sent):

import numpy as np
from concourse.mybir import AluOpType as OP, ActivationFunctionType as AF

W, L, M, RO, N = 4096, 128, 32, 5, 6
XW = W + L
BIG = float(1 << 22)
R1 = float(3 << 22)
R32 = float((1 << 28) + (1 << 23))
R64 = float(3 << 28)
R128 = float(3 << 29)
OFF = 2048.0
CHUNKS = [[(_c[0], int(_c[1])) for _c in _s.split()]
          for _s in ("S2 V1 S3 V1 V1 S2 V1 V1 S1 V1 V1 V1", "S4 V1 S4 V1 V1 V1 V1 S1 V1 V1", "S3 V1 V1 S3 V1 V1 V1 S1 V1 V1 V1 V1")]
NV_ON_S = True
WIDE = False
CY, PCY, GA, SC, WAKE, HOLD = 0.9, 0.45, 1.25, 2.7, 215.0, 230.0
YW, YS = 128, 2
GO, XAB, CF_ON_S, ONEG, WIN_ON_G, XE_ON_V, EX2 = 0, 2, False, True, True, False, True
LOAD, PASSES, LAG, CLS, TOL, MIX = 2700.0, 4, 3800.0, 300.0, 70.0, 0.5
F, B16, F16, I32, U16 = "float32", "bfloat16", "float16", "int32", "uint16"


def _sb(cols, dt_):
    return ("sbuf", [128] + (cols if isinstance(cols, list) else [cols]), dt_)


HALVES = {
    "X": (XW, B16), "win": ((RO + 1) * 128, F), "h16": (32, U16), "wb": (512, B16),
    "sel": (128, B16), "bsel": (128, B16),
    "xab": (128, B16), "sa": (64, F), "ao": (8, U16), "cn": (8, B16),
    "mpq": (128, F16), "spq": (256, F16), "opq": (8, U16), "pq": (8, F), "gg": (8, F), "tr": (32, F16),
    "ci": (128, I32), "cm": (128, I32), "cf": (128, F), "co": (128, U16), "xpq": (128, B16), "yy": (512, B16),
    "dd": (W // 2, B16), "rl": (W // 2, B16), "sk": (256, I32), "ex": (128, B16), "kj": (8, I32),
    "eo": (8, U16), "me": (64, F16), "se": (64, F), "sc": (128, F), "so": (8, U16), "xe": (64, B16),
    "exf": (128, F), "nv": (128, B16), "ni": (128, I32), "ry": (128, F),
}
SCRATCH = {_n: _sb(2 * _v[0], _v[1]) for _n, _v in HALVES.items()}
SCRATCH.update({
    "cmp": _sb([8, 128], B16), "R": _sb([2, 4, 32], F16), "mc": _sb(320, B16),
    "rin": _sb(128, I32), "r16": _sb(128, F16), "wti": _sb(4, I32), "kpi": _sb(4, I32), "kpj": _sb(4, I32),
    "pc": _sb(12, I32), "pf": _sb(20, F), "cex4": _sb(8, U16), "mx": _sb(32, B16), "lc": _sb(64, B16), "bf": _sb(8, F), "j8": _sb(8, F), "jp": _sb(128, B16), "jg": _sb(128, B16),
    "jq": _sb(128, B16), "jc": _sb(128, B16), "j16": _sb(128, B16), "i8": _sb(64, F), "j4": _sb(64, F),
    "i4m": _sb(256, B16), "odd": _sb(64, F), "w4": _sb(8, B16), "wf": _sb(4, F), "kf": _sb(8, F), "km": _sb(64, F16),
    "pk": _sb(8, F), "sl": _sb(8, F), "cs": _sb(8, F), "ch": _sb(8, F), "c1": _sb(64, F), "c2": _sb(64, F), "g0": _sb(128, B16),
    "g1": _sb(128, B16), "g2": _sb(128, B16),
    "idn": _sb([2, 4, 16], B16), "nid": _sb(128, B16), "idf": _sb(128, F), "dm": _sb(128, B16),
    "nb": _sb(128, B16), "bb": _sb(128, B16), "qq": _sb(128, B16), "qc": _sb(256, B16), "qs": _sb(256, B16),
    "tri": _sb(256, B16), "b8": _sb(32, B16), "ca": _sb(128, B16), "rs8": _sb(64, F),
    "rst": _sb(128, B16), "rk": _sb(256, F), "d0": _sb(128, F), "ck": _sb(256, B16), "cexp": _sb(8, U16), "same": _sb(8, U16), "cex2": _sb(8, U16), "b8f": _sb(8, F),
    "one": _sb(128, B16), "half": _sb(128, B16),
    "junk": _sb(16, F), "cnt": _sb(4, F), "aq": _sb(4, F), "ar": _sb(4, F), "ac": _sb(4, F),
})
for _k in range(8):
    SCRATCH["ps%d" % _k] = ("psum", [128, 512], F)

SEMAPHORES = (["cV", "cS", "cP", "cG", "sent", "go"] + ["arr%d" % _t for _t in range(2 * RO)]
              + ["ldx0", "ldx1", "out0", "out1"] + ["dq%d" % _k for _k in range(16)])
COLS = {}
PLAN = {}


def rank_program(g, core, T, topo):
    rank = T.rank_of(core)
    if rank is None:
        return
    ops = []
    ALL = slice(None)
    st = {"cls": 1}

    def A(name, lo=None, hi=None, step=None, part=ALL):
        return (name, (part, slice(lo, hi, step)))

    def half(H):
        def a(name, lo=0, hi=None, step=None, part=ALL):
            n = HALVES[name][0]
            return (name, (part, slice(H * n + lo, H * n + (n if hi is None else hi), step)))
        return a

    def ind(win, off):
        return (win[0], win[1], off)

    def ap(a):
        if not isinstance(a, tuple):
            return a
        v = T[a[0]][a[1]]
        return v.indirect(ap(a[2])) if len(a) == 3 else v

    def add(eng, kind, call, outs, ins, **kw):
        o = {"eng": eng, "kind": kind, "call": call, "outs": outs, "ins": [a for a in ins if isinstance(a, tuple)],
             "dma": False, "after": [], "soft": [], "waits": [], "acc": None, "stop": False, "cls": st["cls"], "sem": None}
        o.update(kw)
        key = (st.get("part"), eng)
        st[key] = st.get(key, 0) + 1
        o["tag"] = st["part"] + (eng, st[key]) if st.get("part") else None
        ops.append(o)
        return len(ops) - 1

    V, S, P = g.vector, g.scalar, g.tensor

    def copy(o, i):
        return add("V", "c", lambda _o: V.tensor_copy(ap(o), ap(i)), [o], [i])

    def tt(o, a, b, op, **kw):
        return add("V", "tt", lambda _o: V.tensor_tensor(ap(o), ap(a), ap(b), op), [o], [a, b], **kw)

    def ts(o, a, s1, op0, s2=None, op1=None):
        if op1 is None:
            return add("V", "c", lambda _o: V.tensor_scalar(ap(o), ap(a), ap(s1), None, op0), [o], [a, s1])
        return add("V", "c", lambda _o: V.tensor_scalar(ap(o), ap(a), ap(s1), ap(s2), op0, op1), [o], [a, s1, s2])

    def scan(o, d0, d1, op0, op1):
        return add("V", "c", lambda _o: V.tensor_tensor_scan(ap(o), ap(d0), ap(d1), 0.0, op0, op1), [o], [d1, d0])

    def fill(o, c):
        return add("V", "c", lambda _o: V.memset(ap(o), c), [o], [])

    def act(o, i, f=AF.Identity, bias=0.0, scale=1.0, acc=None):
        if acc is None:
            return add("S", "a", lambda _o: S.activation(ap(o), ap(i), f, bias=ap(bias), scale=ap(scale)), [o], [i, bias, scale])
        return add("S", "a", lambda _o: S.activation(ap(o), ap(i), f, bias=ap(bias), scale=ap(scale), accum_out=ap(acc)),
                   [o, acc], [i, bias, scale])

    def mm(o, l, r, start, stop, acc=None):
        return add("P", "m", lambda _o: P.matmul(ap(o), ap(l), ap(r), start, _o["stop"]), [o], [l, r], acc=acc, stop=stop)

    def iota(o, pat, base, cm):
        if SCRATCH[o[0]][2] == I32:
            return add("G", "g", lambda _o: g.iota(ap(o), pat, base, cm), [o], [])
        return add("G", "g", lambda _o: g.iota(ap(o), pat, base, cm, allow_small_or_imprecise_dtypes=True), [o], [])

    def dma(q, o, i, sem=None):
        Q = {"Y": g.sync, "S": g.scalar}[q]
        return add(q, "d", lambda _o: Q.dma_start(ap(o), ap(i)), [o] if isinstance(o, tuple) else [], [i], dma=True, sem=sem)

    sent, sends = [0], {}

    def send(H, t):
        a = half(H)
        peer = T.cores[(rank - 1 - t) % N]
        rid, pid, _se = topo.addr(peer)
        es = topo.engines(core, peer)[H::2]
        sent[0] += len(es)
        src, dst = a("win", 128 * t, 128 * t + 64), a("win", 128 * t + 64, 128 * t + 128)

        def call(_o):
            g.remote_dma(ap(dst), ap(src), T.sem["arr%d" % (2 * t + H)], T.sem.sent, pid, rid, sum(1 << e for e in es))
            if (H, t) == (GO, 0):
                g.sem_inc(T.sem.go, 1)

        sends[H, t] = add("G", "r", call, [], [src], dma="remote", first=(H, t) == (0, 0))

    def arrival(H, t):
        return ("arr%d" % (2 * t + H), len(topo.engines(T.cores[(rank + 1 + t) % N], core)[H::2]))

    col = lambda name, j: A(name, j, j + 1)
    IDN = ("idn", (ALL, ALL, ALL, ALL))
    quad = lambda q: slice(32 * q, 32 * q + 32)
    lanes = lambda bank, b0, b1: A(bank, 32 * b0, 32 * b1)
    copy_c = lambda bank, c: A(bank, c, 128, 2)

    def load_x(H):
        for k, (p0, p1) in enumerate(((16, 48), (48, 80), (80, 112), (0, 16), (112, 128))):
            r0 = 64 * H + 16 * (p0 // 32)
            n = dma("YS"[k % 2 * (1 - H)], half(H)("X", 0, W, part=slice(p0, p1)), T.x[r0:r0 + p1 - p0, :], sem="ldx%d" % H)
            if H == 1:
                ops[n]["soft"].append(sends[GO, 0])
                ops[n]["waits"] = [("go", 1)] if k == 0 else []
                if k:
                    ops[n]["soft"].append(n - 1)

    dma("Y", A("rin"), T.ring[:])
    dma("S", A("wti", 0, 1), T.wt[:])
    load_x(0)
    dma("S", A("kpi", 0, 2), T.kap[:])

    iota(col("pc", 0), [[0, 1]], 0, 1)
    iota(A("jp"), [[1, 128]], 0, 0)
    iota(A("jc"), [[16, 4], [0, 2], [1, 16]], 0, 0)
    iota(A("jg"), [[1, 8], [0, 16]], 0, 0)
    iota(A("j16"), [[0, 8], [1, 16]], 0, 0)
    iota(A("jq"), [[1, 4], [0, 32]], 0, 0)
    iota(A("j8"), [[1, 8]], 0, 0)
    iota(A("i8"), [[0, 8], [1, 8]], 0, 0)
    iota(A("j4"), [[0, 2], [1, 4], [0, 8]], 0, 0)
    iota(A("odd"), [[0, 2], [2, 32]], 65, 0)
    iota(A("i4m"), [[0, 8], [4, 32]], 0, 0)
    ts(col("pc", 1), col("pc", 0), 4, OP.arith_shift_right)
    ts(col("pc", 2), col("pc", 0), 15, OP.bitwise_and)
    ts(col("pc", 3), col("pc", 0), 5, OP.arith_shift_right)
    ts(col("pc", 4), col("pc", 0), 4, OP.arith_shift_right, 1, OP.bitwise_and)
    ts(col("pc", 5), col("pc", 0), 1, OP.arith_shift_right, 7, OP.bitwise_and)
    ts(col("pc", 6), col("pc", 0), 3, OP.arith_shift_right, 3, OP.bitwise_and)
    ts(col("pc", 7), col("pc", 0), 7, OP.bitwise_and)
    copy(col("pf", 0), col("pc", 0))
    copy(A("pf", 1, 8), A("pc", 1, 8))
    p_, pg_, r_, q_, hi_, kind_, s7_ = [col("pf", j) for j in (0, 1, 2, 3, 5, 6, 7)]
    ts(IDN, A("jp"), p_, OP.is_equal)
    fill(A("half"), -0.25)
    fill(A("one"), 1.0)
    ts(A("r16"), A("rin"), -OFF, OP.add)
    for q in range(4):
        for ib in range(4):
            mm(A("ps7", ib, 128, 4, part=quad(q)), A("r16", 32 * ib, 32 * ib + 32), ("idn", (ALL, ALL, q, ALL)), True, True)
    for H in range(2):
        act(half(H)("win", 0, 64), A("ps7", 64 * H, 64 * H + 64))
        send(H, 0)
        ts(half(H)("h16", 4 * RO, 4 * RO + 8), half(H)("win", 0, 8), OFF, OP.add)
    load_x(1)
    ts(col("pf", 8), p_, -64.0, OP.add)
    ts(col("pf", 9), pg_, -4.0, OP.add)
    ts(col("w4", 0), col("wti", 0), 4.0, OP.mult)
    ts(A("bb"), A("jg"), pg_, OP.is_equal)
    ts(A("dm"), A("j16"), r_, OP.is_equal)
    fill(A("wb"), 0.0)
    for H in range(2):
        ts(half(H)("sel"), A("jc"), (p_, col("pf", 8))[H], OP.is_equal)
        ts(half(H)("bsel"), A("jq"), (pg_, col("pf", 9))[H], OP.is_equal)
        mm(col("ps4", H), half(H)("sel"), col("w4", 0), True, True)
    act(A("wf", 0, 2), A("ps4", 0, 2))
    act(A("wf", 2, 4), A("ps4", 0, 2), scale=-1.0)
    for H in range(2):
        for k in range(4):
            act(half(H)("wb", 128 * k + k % 2, 128 * k + 128, 2), A("bb", k % 2, 128, 2), scale=col("wf", H + 2 * (k // 2)))
    ts(A("c1"), A("i8"), hi_, OP.not_equal, -BIG, OP.mult)
    tt(A("ca", 64, 128), A("c1"), A("j4"), OP.add)
    ts(A("ca", 0, 64), A("j4"), -1.0, OP.mult, 63.5, OP.add)
    ts(A("rs8"), A("i8"), 1.0, OP.min)
    for k, c in enumerate((R128, 2 * R128, 127.5)):
        act(A("mc", 64 * k, 64 * k + 64), A("one", 0, 64), scale=c)
    act(A("mc", 192, 320), A("one"), scale=R1)
    act(A("rst"), A("one"))
    act(A("rst", 0, 128, 16), A("one", 0, 8), scale=0.0)
    ts(A("kpj", 0, 2), A("kpi", 0, 2), 1, OP.bitwise_and)
    ts(A("kf", 0, 2), A("kpi", 0, 2), 1984.0, OP.is_gt, -4096.0, OP.mult)
    ts(A("kf", 2, 4), A("kpi", 0, 2), 64.0, OP.add)
    tt(A("kf", 4, 6), A("kf", 0, 2), A("kf", 2, 4), OP.add)
    ts(A("kf", 6, 8), A("kpj", 0, 2), OFF, OP.mult, 31.0 - OFF, OP.add)
    for k in range(4):
        ts(A("km", 16 * k, 16 * k + 16), A("dm", 0, 16), col("kf", 4 + k), OP.mult)
    for H in range(2):
        for k in range(2):
            mm(lanes("ps5", 2 * k + H, 2 * k + H + 1), half(H)("bsel"), A("km", 32 * k, 32 * k + 32), True, True)
    ts(A("pk"), A("j8"), kind_, OP.is_equal)
    ts(A("sl"), A("j8"), s7_, OP.is_equal)
    ts(A("cs"), A("j8"), col("pf", 4), OP.is_equal)
    ts(A("ch"), A("j8"), col("pf", 4), OP.is_equal, 0.5, OP.mult)
    act(A("odd"), A("odd"), scale=col("pk", 1))
    act(A("c1"), lanes("ps5", 0, 2), scale=col("pk", 0))
    act(A("c2"), lanes("ps5", 2, 4), scale=col("pk", 2))
    tt(A("c1"), A("c1"), A("c2"), OP.add)
    tt(A("c2"), A("c1"), A("odd"), OP.add)
    for ib in range(4):
        ts(("R", (ALL, ALL, ib, ALL)), A("c2"), col("sl", 2 * ib + 1), OP.mult)
    fill(A("sk"), 0)
    for H in range(2):
        copy(half(H)("spq", 128, 256), A("one"))
        fill(half(H)("X", W, XW), 0.0)
    act(A("nid"), IDN, scale=-1.0)
    act(A("idf"), IDN)
    for c in range(2):
        act(copy_c("nb", c), A("dm", 0, 64), bias=BIG, scale=-BIG)
    for k, s in enumerate((128.0, 256.0, -128.0, 1.0)):
        act(A("b8", 8 * k, 8 * k + 8), A("bb", 0, 128, 16), scale=s)
    act(A("bf"), A("bb", 0, 128, 16))
    ts(A("ck"), A("i4m"), pg_, OP.add)
    fill(A("rk"), 0.0)
    act(A("rk", 0, 256, 32), A("one", 0, 8), scale=BIG)
    act(A("d0"), A("one"), scale=-2 * OFF)
    ts(col("pf", 10), r_, W - OFF, OP.add)
    ts(A("d0", 0, 128, 16), A("j8"), 16.0, OP.mult, col("pf", 10), OP.add)
    copy(A("cexp"), A("j8"))
    if EX2:
        ts(col("pc", 8), col("pc", 0), 2, OP.arith_shift_right, 3, OP.bitwise_and)
        copy(col("pf", 16), col("pc", 8))
        ts(A("cex4", 0, 2), A("j8", 0, 2), 4.0, OP.mult, col("pf", 16), OP.add)
        for k in range(4):
            act(A("mx", k, 32, 4), A("one", 0, 8), scale=col("bf", k))
        act(A("lc"), A("one", 0, 64), scale=0.0)
        for k in (0, 48):
            act(A("lc", k, k + 16), A("dm", 0, 16))
    ts(A("same"), A("j8"), 16.0, OP.mult, r_, OP.add)
    if WIDE:
        ts(A("cex2"), A("j8"), 16.0, OP.mult, 15.0, OP.add)
        for m2 in range(2):
            act(A("b8f", m2, 8, 2), A("bb", 64 * m2, 64 * m2 + 64, 16))
    ts(A("qq"), A("jq"), q_, OP.is_equal)
    ts(col("pf", 11), q_, 16.0, OP.mult, r_, OP.add)
    ts(col("pf", 12), q_, 16.0, OP.mult, 15.0, OP.add)
    ts(col("pf", 13), col("cs", 1), 99.0, OP.mult, col("pf", 11), OP.add)
    ts(col("pf", 14), q_, 16.0, OP.mult, -1.0, OP.add)
    ts(col("pf", 15), r_, 1.0, OP.add, col("cs", 1), OP.mult)
    tt(col("pf", 14), col("pf", 14), col("pf", 15), OP.add)
    for c in range(2):
        act(A("qc", 128 * c, 128 * c + 128), A("qq"), scale=col("cs", c))
        ts(A("qs", 128 * c, 128 * c + 128), A("jc"), col("pf", 11), OP.is_equal, col("ch", c), OP.mult)
    ts(A("g0"), A("jc"), col("pf", 13), OP.is_gt)
    ts(A("g1"), A("jc"), col("pf", 14), OP.is_gt)
    tt(A("tri", 0, 128), A("g0"), A("qq"), OP.mult)
    tt(A("tri", 128, 256), A("g1"), A("qq"), OP.mult)

    sbank = [0]

    def pre(H, t):
        a = half(H)
        st["cls"], st["part"] = 1, (H, t, "pre")
        X, w0, h0 = a("X", 0, W), 128 * t, 4 * (RO - t)
        own = "ps%d" % (2 + H)
        PA, PY, PS = A(own, 0, 64), A("ps4", 0, 64), lambda *s, **k: A("ps7", *s, **k)
        dma("Y", a("win", w0 + 132, w0 + 192), a("win", w0, w0 + 60), sem="dq%d" % (3 + 2 * t + H))
        if XAB == 2:
            copy(a("xab", 0, 64), ind(X, a("h16", h0, h0 + 4)))
            act(a("xab", 64, 128), ind(X, a("h16", h0 + 4, h0 + 8)))
        elif XAB == 1:
            copy(a("xab"), ind(X, a("h16", h0, h0 + 8)))
        else:
            act(a("xab"), ind(X, a("h16", h0, h0 + 8)))
        mm(PA, IDN, A("ca", 0, 64), True, False)
        for k in (2, 3):
            mm(PA, a("wb", 128 * k, 128 * k + 128), a("xab", k % 2, 128, 2), False, False)
        mm(PA, IDN, A("mc", 0, 64), False, False)
        mm(PA, A("nid"), A("mc", 0, 64), False, False)
        for k in (0, 1):
            mm(PA, a("wb", 128 * k, 128 * k + 128), a("xab", k % 2, 128, 2), False, False)
        mm(PA, IDN, A("ca", 64, 128), False, True)
        scan(a("sa"), A("rs8"), PA, OP.mult, OP.max)
        copy(a("ao"), a("sa", 7, 64, 8))
        tt(a("mpq"), ind(a("win", w0, w0 + 128), a("ao")), A("dm"), OP.mult, waits=[arrival(H, t)], after=[sends[H, t]])
        scan(a("spq", 0, 128), A("rst"), a("mpq"), OP.mult, OP.add)
        add("V", "c", lambda _o: V.transpose(ap(a("tr")), ap(a("spq", 7, 256, 8))), [a("tr")], [a("spq", 7, 256, 8)])
        tt(a("pq", 0, 4), a("spq", 15, 64, 16), a("spq", 79, 128, 16), OP.mult)
        ts(a("opq"), a("spq", 15, 128, 16), OFF, OP.add)
        for k, bank in enumerate(("ps7", own)):
            for q in range(4):
                n = mm(A(bank, 0, 64, part=quad(q)), a("tr", part=quad(q)), ("R", (quad(q), H, slice(2 * k, 2 * k + 2), ALL)), True, True)
                if k:
                    ops[n]["soft"].append(n - 1)
        ts(a("gg", 0, 4), a("pq", 0, 4), -1007.5 if t == 0 else col("ac", t % 2), OP.add, R32, OP.add)
        act(a("xpq"), ind(X, a("opq")))
        mm(PY, IDN, A("mc", 128, 192), True, False)
        for k, l in enumerate((A("nid"), IDN)):
            mm(PY, l, a("xpq", 0, 64), False, False)
            mm(PY, l, a("xpq", 64, 128), False, k == 1)
            if k == 0:
                mm(PY, IDN, A("mc", 64, 128), False, False)
                mm(PY, A("nid"), A("mc", 64, 128), False, False)
        for ib in range(4):
            ts(a("ci", ib, 128, 4), lanes(("ps7", own)[ib // 2], ib % 2, ib % 2 + 1), 32.0, OP.mult, a("gg", ib, ib + 1), OP.add)
        for k in range(2):
            ts(a("cm", 64 * k, 64 * k + 64), a("ci", 64 * k, 64 * k + 64), 5, OP.arith_shift_right, W - 1, OP.bitwise_and)
        for k in range(2):
            copy(a("co", 64 * k, 64 * k + 64), a("cm", 64 * k, 64 * k + 64))
        for k in range(YS):
            act(a("yy", 64 * k, 64 * k + 64), PY)
        for k in range(64 * YS, YW, 128):
            copy(a("yy", k, k + 128), a("yy", 0, 128))
        st["cls"] = 0
        if CF_ON_S:
            act(a("cf"), ind(a("cm"), A("same")), bias=-OFF)
        else:
            ts(a("cf"), a("cm"), -OFF, OP.add)
        if t < RO - 1:
            act(a("cn"), a("sa", 7, 64, 8), AF.Sign, bias=-63.5)
            mm(PS(256 + 8 * H, 264 + 8 * H), A("one"), a("cn"), True, True)
            if H == 1:
                act(A("junk"), PS(256, 272), bias=64 - (31 + 15.5 / 32) / 16, scale=0.5, acc=col("cnt", 0))
                act(col("aq", 0), col("cnt", 0), bias=R64)
                act(col("ar", 0), col("aq", 0), bias=32 * R64, scale=-32.0)
                act(col("ac", (t + 1) % 2), col("cnt", 0), bias=col("ar", 0), scale=32.0)

    def score(H, t):
        a = half(H)
        X, bank, grp = a("X", 0, W), "ps%d" % (2 + H), (H, t)
        st["cls"], st["part"] = 1, (H, t, "score")
        low = slice(0, 64)
        if WIDE:
            mm(A(bank, 0, 128), IDN, A("ck", 0, 256, 2), True, False)
        else:
            mm(A(bank, 0, 256, part=low), ("idn", (ALL, 0, ALL, ALL)), A("ck"), True, False)
        st["cls"] = 0
        line = {}

        def turn(who, n):
            if who in line:
                ops[n]["soft"].append(line[who])
            line[who] = n

        def keys(buf, p0, n, c):
            for mp in range(p0, p0 + n) if WIDE else ():
                mm(A(bank, mp, 128, 16), a(buf, 128 * mp, 128 * mp + 128), A("b8", c, c + 8), False, False, acc=grp)
            for m in () if WIDE else range(2 * p0, 2 * (p0 + n)):
                mm(A(bank, m, 256, 32, part=low), a(buf, 64 * m, 64 * m + 64), A("b8", c, c + 8), False, False, acc=grp)

        def first(who, p0, n, sb):
            lo, hi = 128 * p0, 128 * (p0 + n)
            if who == "W":
                for k in range(n):
                    turn("V", tt(a("dd", lo + 128 * k, lo + 128 * k + 128), ind(X, a("co", 8 * (p0 + k), 8 * (p0 + k + 1))),
                                 a("yy", 0, 128), OP.subtract))
            elif who == "V":
                turn(who, tt(a("dd", lo, hi), ind(X, a("co", 8 * p0, 8 * (p0 + n))), a("yy", 0, hi - lo), OP.subtract))
                keys("dd", p0, n, 16)
            else:
                turn(who, act(a("dd", lo, hi), ind(X, a("co", 8 * p0, 8 * (p0 + n)))))
                for k in range(0, hi - lo, YW):
                    e = min(k + YW, hi - lo)
                    mm(A(sb, k, e), A("nid"), a("yy", 0, e - k), k == 0 or not ONEG, False)
                    if not ONEG:
                        mm(A(sb, k, e), IDN, a("dd", lo + k, lo + e), False, True)
                if ONEG:
                    mm(A(sb, 0, hi - lo), IDN, a("dd", lo, hi), False, True)

        def second(who, p0, n, sb):
            lo, hi = 128 * p0, 128 * (p0 + n)
            if who == "W":
                act(a("rl", lo, hi), a("dd", lo, hi), AF.Abs)
                keys("rl", p0, n, 0)
            elif who == "V":
                turn(who, ts(a("rl", lo, hi), a("dd", lo, hi), 0.0, OP.max))
                keys("rl", p0, n, 8)
            else:
                turn(who, act(a("rl", lo, hi), A(sb, 0, hi - lo), AF.Abs))
                keys("rl", p0, n, 0)

        p0, due = 0, {}
        for who, n in CHUNKS[2 if (H, t) == (1, RO - 1) else H]:
            sbank[0] += who == "S"
            job = (who, p0, n, "ps%d" % (sbank[0] % 2))
            first(*job)
            if who in due:
                second(*due[who])
            due[who] = job
            p0 += n
        for job in due.values():
            second(*job)

    def post(H, t):
        a = half(H)
        st["cls"], st["part"] = 1, (H, t + 1, "post")
        last = t == RO - 1
        X, w1, h1, bank = a("X", 0, W), 128 * (t + 1), 4 * (RO - t - 1), "ps%d" % (2 + H)
        low = slice(0, 64)
        if WIDE:
            scan(a("sk", 0, 128), A("rk", 0, 256, 2), A(bank, 0, 128), OP.add, OP.min)
            tt(a("exf"), ind(a("sk", 0, 128), A("cex2")), A("dm"), OP.mult)
            mm(A(bank, 128, 136), a("exf"), A("b8f"), True, True)
            scan(a("sk", 128, 136), A("rk", 0, 128, 16), A(bank, 128, 136), OP.add, OP.min)
            ts(a("kj", 0, 4), a("sk", 129, 136, 2), 127, OP.bitwise_and)
            copy(a("eo", 0, 4), a("kj", 0, 4))
        else:
            scan(a("sk", part=low), A("rk", part=low), A(bank, 0, 256, part=low), OP.add, OP.min)
            ts(a("kj"), a("sk", 31, 256, 32), 127, OP.bitwise_and)
            if EX2:
                tt(a("ex", 0, 32), ind(a("kj"), A("cex4", 0, 2)), A("mx"), OP.mult)
                for q in range(4):
                    for c in range(2):
                        j = 8 * q + 4 * c
                        mm(A(bank, 256, 260, part=quad(q)), A("lc", 32 * c, 32 * c + 32, part=low), a("ex", j, j + 4, part=low), c == 0, c == 1)
            else:
                tt(a("ex"), ind(a("kj"), A("cexp")), A("dm"), OP.mult)
                mm(A(bank, 256, 260), a("ex"), A("b8", 24, 28), True, True)
            copy(a("eo", 0, 4), A(bank, 256, 260))
        mm(lanes("ps5", 0, 4), IDN, A("nb"), True, False)
        mm(lanes("ps6", 0, 4), IDN, A("half"), True, False)
        for c in range(2):
            mm(lanes("ps6", 2 * c, 2 * c + 2), A("qs", 128 * c, 128 * c + 128), a("yy", 0, 64), False, False)
        me, e = a("me"), a("se", 15, 64, 16)
        tt(me, ind(a("cf"), a("eo", 0, 4)), A("dm", 0, 64), OP.mult)
        for c in range(2):
            mm(copy_c(bank, c), A("qc", 128 * c, 128 * c + 128), me, True, True)
        scan(a("se"), A("rst", 0, 64), me, OP.mult, OP.add)
        ts(a("h16", h1, h1 + 4), e, OFF, OP.add)
        for c in range(2):
            mm(copy_c("ps5", c), A("qc", 128 * c, 128 * c + 128), me, False, False)
        if WIN_ON_G:
            new = a("win", w1, w1 + 4)
            add("G", "g", lambda _o: g.affine_select(ap(new), ap(e), [[0, 4]], OP.is_ge, 0.0, 0, 0), [new], [e])
        else:
            act(a("win", w1, w1 + 4), e)
        if not last:
            send(H, t + 1)
        (copy if XE_ON_V else act)(a("xe"), ind(X, a("h16", h1, h1 + 4)))
        for c in range(2):
            mm(lanes("ps6", 2 * c, 2 * c + 2), A("qs", 128 * c, 128 * c + 128), a("xe"), False, c == 1 and not NV_ON_S)
        if NV_ON_S:
            mm(lanes("ps6", 0, 4), IDN, A("mc", 192, 320), False, False)
            mm(lanes("ps6", 0, 4), A("nid"), A("mc", 192, 320), False, True)
        for ib in range(4):
            ts(("cmp", (ALL, 4 * H + ib, slice(0, 128 - 32 * ib))), lanes(bank, ib, 4), a("se", 16 * ib + 15, 16 * ib + 16),
               OP.is_equal, 8192.0, OP.mult)
            if ib < 3:
                mm(lanes("ps5", ib + 1, 4), A("qq"), ("cmp", (ALL, 4 * H + ib, slice(32, 128 - 32 * ib))), False, False)
        for c in range(2):
            mm(copy_c("ps5", c), A("tri", 128 * c, 128 * c + 128), ("cmp", (ALL, slice(4 * H, 4 * H + 4), slice(c, 32, 2))), False, c == 1)
        if NV_ON_S:
            act(a("nv"), lanes("ps6", 0, 4))
        else:
            copy(a("ni"), lanes("ps6", 0, 4))
        for c in range(2):
            scan(a("sc", 64 * c, 64 * c + 64), A("d0", 64 * c, 64 * c + 64), copy_c("ps5", c), OP.max, OP.min)
        ts(a("so"), a("sc", 15, 128, 16), OFF, OP.add)
        copy(ind(a("X"), a("so")), a("nv" if NV_ON_S else "ni"))
        if last:
            for k in range(2):
                r0 = 64 * H + 32 * k
                dma("Y", T.yx[r0:r0 + 32, :], a("X", 0, W, part=slice(64 * k + 16, 64 * k + 48)), sem="out%d" % H)
            mm(A(bank, 256, 384, part=slice(0, 64)), a("win", w1, w1 + 64), A("idf"), True, True)
            act(a("ry", part=slice(0, 64)), A(bank, 256, 384, part=slice(0, 64)), bias=OFF)
            for q in range(4):
                r0 = 16 * (4 * H + q)
                dma("S", T.yr[r0:r0 + 16, :], a("ry", 32 * q, 32 * q + 32, part=slice(0, 64)), sem="out%d" % H)

    pre(0, 0)
    score(0, 0)
    pre(1, 0)
    for t in range(RO):
        post(0, t)
        score(1, t)
        if t < RO - 1:
            pre(0, t + 1)
        post(1, t)
        if t < RO - 1:
            score(0, t + 1)
            pre(1, t + 1)

    if not PLAN:
        loads = [n for n, o in enumerate(ops) if o["dma"] is True][:8]
        for k, n in zip(loads, loads[1:]):
            ops[n]["soft"].append(k)
        PLAN["deps"], PLAN["order"] = arrange(ops)
    emit(g, T, ops, PLAN["deps"], PLAN["order"], sent[0])


def touched(a):
    key = (a[0], repr(a[1][1:]))
    if key not in COLS:
        m = np.zeros(SCRATCH[a[0]][1][1:], bool)
        m[a[1][1:]] = True
        COLS[key] = int.from_bytes(np.packbits(m.reshape(-1)).tobytes(), "big")
    return COLS[key]


def arrange(ops):
    seen, deps, dur, lat = {}, [], [], []
    for n, o in enumerate(ops):
        rd = [(x[0], touched(x)) for x in o["ins"]] + [(x[2][0], touched(x[2])) for x in o["ins"] + o["outs"] if len(x) == 3]
        wr = [(x[0], touched(x)) for x in o["outs"]]
        d = set(o["after"])
        for w, lst in ((False, rd), (True, wr)):
            for name, m in lst:
                runs = []
                for (k, km, kw) in reversed(seen.get(name, [])):
                    if name.startswith("ps"):
                        if not runs or runs[-1] != (ops[k]["eng"], ops[k]["acc"]):
                            runs.append((ops[k]["eng"], ops[k]["acc"]))
                            if len(runs) > 2:
                                break
                        if ops[k]["eng"] != o["eng"] or (o["eng"] == "P" and (o["acc"] is None or o["acc"] != ops[k]["acc"])):
                            d.add(k)
                    elif (kw or w) and not (o["dma"] and o["sem"] and o["sem"] == ops[k]["sem"]) and m & km:
                        d.add(k)
        for w, lst in ((False, rd), (True, wr)):
            for name, m in lst:
                seen.setdefault(name, []).append((n, m, w))
        deps.append(d)
        size = lambda x: 16 * touched(x[2]).bit_count() if len(x) == 3 else touched(x).bit_count()
        two = all(SCRATCH[x[0]][2] in (B16, F16, U16) for x in o["outs"] + o["ins"] if size(x) > 1)
        k, extra = o["kind"], 0.0
        if k == "d":
            x = (o["outs"] + o["ins"])[0]
            t_, extra = 60.0, 1800.0 + {"ldx0": LOAD, "ldx1": LOAD}.get(o["sem"], 0.0)
        elif k == "r":
            t_, extra = 300.0, 3500.0 if o["first"] else 2000.0
        elif k == "m":
            t_ = PCY * max(min(64, size(o["ins"][0])), size(o["ins"][1])) * (4 if SCRATCH[o["ins"][0][0]][2] == F else 1)
        elif k == "g":
            t_ = 150 + 2 * CY * size(o["outs"][0])
        elif len(o["outs"][0]) == 3:
            t_ = 55 + SC * size(o["outs"][0])
        elif o["ins"] and len(o["ins"][0]) == 3:
            t_ = 60 + GA * size(o["outs"][0])
        else:
            both = k == "tt" and not any(x[0].startswith("ps") for x in o["ins"])
            t_ = CY * max(64, size(o["outs"][0]) * (2 if both else 0.5 if two and k == "c" else 1)) + (30 if k == "a" else 0)
        dur.append(t_)
        lat.append(extra)
    hard = deps
    deps = [d | set(o["soft"]) for d, o in zip(hard, ops)]
    wait = lambda k, n: 0.0 if ops[k]["eng"] == ops[n]["eng"] == "P" or k not in hard[n] else lat[k] + WAKE
    users = [[] for _ in ops]
    for n, d in enumerate(deps):
        for k in d:
            users[k].append(n)
    rest = [0.0] * len(ops)
    tail = list(lat)
    choice = [[n for n, o in enumerate(ops) if o["tag"] == (H, RO, "post", "V", 1)][0] for H in range(2)]
    for _ in range(2):
        for n in range(len(ops) - 1, -1, -1):
            rest[n] = dur[n] + max([wait(n, u) + rest[u] for u in users[n]] + [tail[n]])
        tail[choice[0]] = rest[choice[1]] - dur[choice[1]] + LAG
    before = [[(k, wait(k, n)) for k in d] for n, d in enumerate(deps)]
    behind = [[(u, wait(n, u)) for u in users[n]] for n in range(len(ops))]

    def place(turn, needs, lead):
        end, busy = [0.0] * len(ops), {e: [] for e in "VSPGY"}
        for n in turn:
            t0 = max([end[k] + w for k, w in needs[n]] + [lead[n]])
            b = busy[ops[n]["eng"]]
            j = len(b)
            while j and b[j - 1][1] > t0:
                j -= 1
            while j < len(b) and t0 + dur[n] > b[j][0]:
                t0 = max(t0, b[j][1])
                j += 1
            b.insert(j, (t0, t0 + dur[n]))
            end[n] = t0 + dur[n]
        return end

    def greedy(rank, needs, gives, lead):
        left, ready, end = [len(d) for d in needs], list(lead), [0.0] * len(ops)
        avail = {e: [n for n, o in enumerate(ops) if o["eng"] == e and not needs[n]] for e in "VSPGY"}
        free, order = {e: 0.0 for e in avail}, []
        while len(order) < len(ops):
            e = min((e for e in avail if avail[e]), key=lambda e: max(free[e], min(ready[n] for n in avail[e])))
            t0 = max(free[e], min(ready[n] for n in avail[e]))
            n = max((n for n in avail[e] if ready[n] <= t0 + HOLD), key=lambda n: rank[n])
            if ready[n] > t0:
                fit = [k for k in avail[e] if ready[k] <= t0 and t0 + dur[k] <= ready[n] + TOL]
                if fit:
                    n = max(fit, key=lambda n: rank[n])
            avail[e].remove(n)
            end[n] = free[e] = max(t0, ready[n]) + dur[n]
            order.append(n)
            for u, w in gives[n]:
                ready[u] = max(ready[u], free[e] + w)
                left[u] -= 1
                if not left[u]:
                    avail[ops[u]["eng"]].append(u)
        return order, end

    calls, none, best = range(len(ops)), [0.0] * len(ops), None
    rank = [rest[n] + CLS * ops[n]["cls"] for n in calls]
    for _ in range(PASSES):
        order, end = greedy(rank, before, behind, none)
        span = max(end[n] + lat[n] for n in calls)
        if best is None or span < best[0]:
            best = (span, order)
        back = greedy(end, behind, before, tail)[1]
        rank = [MIX * back[n] + (1 - MIX) * rank[n] for n in calls]
    PLAN["span"] = best[0]
    PLAN["dbg"] = (ops, rest, behind, dur, greedy, before, tail)
    return hard, best[1]


def emit(g, T, ops, deps, order, sent):
    Q = {"V": g.vector, "S": g.scalar, "P": g.tensor, "G": g, "Y": g.sync}
    know, seq, total, ndma, lastacc = {k: {} for k in Q}, {k: 0 for k in Q}, {}, 0, {}
    for n in order:
        o = ops[n]
        if o["acc"]:
            lastacc[o["acc"]] = n
        if o["dma"] is True:
            if not o["sem"]:
                o["sem"] = "dq%d" % ndma
                ndma += 1
            total[o["sem"]] = total.get(o["sem"], 0) + 16
    for n in lastacc.values():
        ops[n]["stop"] = True
    for n in order:
        o = ops[n]
        e = o["eng"]
        need = {}
        for k in deps[n]:
            if ops[k]["dma"] == "remote" or (e == "P" and ops[k]["eng"] == "P"):
                continue
            key, val = ops[k]["id"]
            if know[e].get(key, 0) < val and need.get(key, (0, 0))[0] < val:
                need[key] = (val, k)
        for key in list(need):
            val, k = need[key]
            if any(k2 != k and ops[k2]["done"].get(key, 0) >= val for (_v, k2) in need.values()):
                del need[key]
        o["need"] = [k for (_v, k) in need.values()]
        for k in o["need"]:
            ops[k]["signal"] = True
            for key, val in ops[k]["done"].items():
                if know[e].get(key, 0) < val:
                    know[e][key] = val
        if o["dma"] == "remote":
            o["id"] = None
        elif o["dma"]:
            o["id"] = (o["sem"], 1)
        else:
            seq[e] += 1
            o["id"] = ("c" + e, seq[e])
        o["done"] = dict(know[e])
        if o["id"]:
            o["done"][o["id"][0]] = o["id"][1]
    count, waited = {k: 0 for k in Q}, set()
    for n in order:
        o = ops[n]
        q = Q[o["eng"]]
        for k in o["need"]:
            q.wait_ge(T.sem[ops[k]["id"][0]], ops[k]["val"])
            waited.add(ops[k]["id"][0])
        for name, val in o["waits"]:
            q.wait_ge(T.sem[name], val)
        r = o["call"](o)
        if o["dma"] == "remote":
            continue
        if o["dma"]:
            o["val"] = total[o["sem"]]
            r.then_inc(T.sem[o["sem"]], 16)
        elif o.get("signal"):
            count[o["eng"]] += 1
            o["val"] = count[o["eng"]]
            r.then_inc(T.sem[o["id"][0]], 1)
    g.wait_ge(T.sem.sent, sent)
    for name, val in total.items():
        if name not in waited:
            g.wait_ge(T.sem[name], val)
